import numpy as np, ml_dtypes
CORES = [242,247,114,119]
N = 4
BF = ml_dtypes.bfloat16
def gentries(a):
    return np.ascontiguousarray(a.reshape(8, 16, -1).transpose(0, 2, 1)).reshape(8, -1)
def gtable(e):
    e = np.asarray(e); return np.ascontiguousarray(e.reshape(8, -1, 16).transpose(0, 2, 1)).reshape(128, -1).astype(np.int32)
V, G, D, S, RO = 2048, 256, 2, 8, 3
def parts(rng):
    o = np.argsort(rng.random((N, 8, V)), axis=2); pos = np.argsort(o, axis=2)
    x = rng.integers(0, 256, (N, 8, 16, 1)) + np.add.accumulate(rng.integers(-100, 101, (N, 8, 16, V)), axis=3)
    phi = np.take_along_axis(x, pos[:, :, None, :], 3) & 255
    nb = np.stack([np.take_along_axis(o, (pos + j) % V, 2) for j in (-1, 1, -32, 32)[:D]], 2)
    snd = np.argsort(rng.random((N, 8, V)), axis=2)[..., :G]
    return phi, nb, np.ascontiguousarray(snd)
def mix(rng, nb, own, ghost):
    z = rng.random(nb.shape)
    nb = np.where(z < ghost, rng.integers(V, V + G, nb.shape), np.where(z < ghost + own, rng.integers(0, V, nb.shape), nb))
    return np.take_along_axis(nb, np.argsort(rng.random(nb.shape), axis=2), 2)
def pack(phi, nb, snd):
    return {"phi": np.ascontiguousarray(phi.reshape(N, 128, V)).astype(np.float32).astype(BF), "nb": np.ascontiguousarray(nb.reshape(N, 8, D * V)).astype(np.int32),
            "snd": np.stack([gtable(a) for a in snd])}
def setup_inputs(rng):
    phi, nb, snd = parts(rng)
    own = rng.choice(np.array([0.0, 0.05, 0.15, 0.3]), (N, 8, 1, 1)); ghost = rng.choice(np.array([0.02, 0.05, 0.1, 0.2]), (N, 8, 1, 1))
    return pack(phi, mix(rng, nb, own, ghost), snd)
def setup_inputs_chains(rng):
    phi, nb, snd = parts(rng); v = np.arange(V); lens = [S, S + 1, S + 2, 2 * S + 1, 3 * S, S * S + 1, V, 5]
    steep = rng.random((N, 8, 16, 1)) < 0.5; steep[np.arange(N), (6 - np.arange(N)) % 8, :8] = True
    step = np.where(steep, rng.choice(np.array([-1, 1]), (N, 8, 16, 1)) * rng.integers(100, 128, (N, 8, 16, V)), rng.integers(-100, 101, (N, 8, 16, V)) + rng.integers(-27, 28, (N, 8, 16, 1)))
    phi = (rng.integers(0, 256, (N, 8, 16, 1)) + np.add.accumulate(step, axis=3)) & 255
    for q in range(N):
        for g in range(8):
            b = lens[(g + q) % 8]; head = v - v % b
            down = np.maximum(v - 1, head); up = np.minimum(np.minimum(v + 1, head + b - 1), V - 1)
            nb[q, g] = np.stack([down, up, v, down][:D])
            h = v[v % b == 0][1::2]; nb[q, g, D - 1, h] = rng.integers(V, V + G, len(h))
    return pack(phi, mix(rng, nb, 0.0, 0.0), snd)
def steep_sums(rng, n):
    return np.concatenate([np.zeros((16, 1), np.int64), np.add.accumulate(rng.integers(122, 128, (16, n)), axis=1)], axis=1)
def deep(rng, phi, nb, snd, g):
    T = S * (S + 1); t = np.arange(T + 1); root = t % (S + 1) == 0; slot = rng.integers(0, G, N); last = np.zeros((N, 16, 1), np.int64)
    sign = np.where(np.argsort(rng.random((N, 16, 1)), axis=1) < 8, 1, -1)
    for q in range(N):
        w = np.sort(rng.permutation(V // 2)[:T + 1]); a = np.zeros(T + 1, np.int64)
        a[root] = w[:S + 1]; a[~root] = w[S + 1:]
        y = rng.integers(0, 256, (16, 1)) + sign[q] * steep_sums(rng, T)
        phi[q, g][:, a] = y & 255; last[q] = y[:, T:] & 255
        lo = np.concatenate([a[:1], a[:-1]]); nb[q, g][:, a] = np.stack([lo, a, lo, a][:D]); snd[q, g, slot[q]] = a[T]
    for q in range(N):
        w = V // 2 + np.sort(rng.permutation(V // 2)[:(S + 1) * (S + 1)]); o = (q - 1) % N
        b = np.zeros(T + 1, np.int64); b[0] = V + slot[o]
        b[1:][root[1:]] = np.concatenate([w[:S - 1], w[2 * S:2 * S + 1]]); b[1:][~root[1:]] = w[2 * S + 1:]
        y = last[o] + sign[o] * steep_sums(rng, T); phi[q, g][:, b[1:]] = y[:, 1:] & 255
        nb[q, g][:, b[1:]] = np.stack([b[:-1], b[1:], b[:-1], b[1:]][:D])
        z = w[S - 1:2 * S]; y = rng.integers(0, 256, (16, 1)) - sign[o] * steep_sums(rng, S); phi[q, g][:, z] = y & 255
        lo = np.concatenate([z[S:], z[:-1]]); hi = np.concatenate([z[S:], z[1:S], b[T:]])
        nb[q, g][:, z] = np.stack([lo, hi, lo, hi][:D])
def late(rng, nb, g):
    J = 3 * S; F = J + 2; P = S * S + S + 1; M = 3 * F + P + 4; j = np.arange(F)
    path = np.concatenate([np.array([J - 1]), 3 * F + np.arange(S), 3 * F + np.arange(S + 1, P), np.array([M - 1])])
    lo = np.arange(M); hi = np.arange(M)
    lo[:F] = F + j; hi[:F] = F + j; lo[J:F] = j[J:]
    lo[F:2 * F] = j; hi[F + 1:2 * F] = 2 * F + j[:-1]; lo[2 * F:3 * F] = j
    lo[path[1:]] = path[:-1]
    c = 3 * F + S; lo[c] = M - 4; hi[c] = M - 4; lo[M - 4] = M - 1; hi[M - 4] = M - 1
    lo[M - 3] = M - 2; hi[M - 3] = M - 2; lo[M - 2] = M - 3; hi[M - 2] = M - 1
    for q in range(N):
        w = np.sort(rng.permutation(V)[:M]); nb[q, g][:, w] = np.stack([w[lo], w[hi], w[lo], w[hi]][:D])
def setup_inputs_loops(rng):
    phi, nb, snd = parts(rng); nb = mix(rng, nb, 0.1, rng.choice(np.array([0.02, 0.05, 0.1]), (N, 8, 1, 1)))
    far = S * S; J = min(S + 2, V // (1 + S + far)); M = J * (1 + S + far)
    ids = np.sort(np.argsort(rng.random((N, 8, V)), axis=2)[..., :M], axis=2)
    j = np.arange(J).reshape(J, 1); br = J + S * j + np.arange(S); pa = J + J * S + far * j + np.arange(far)
    lo = np.concatenate([br[:, S - 1], np.concatenate([j, br[:, :-1]], axis=1).reshape(-1), np.concatenate([j, pa[:, :-1]], axis=1).reshape(-1)])
    hi = np.arange(M); hi[:J] = br[:, S - 1]; hi[br[1:, S - 1]] = pa[:-1, far - 1]
    step = rng.choice(np.array([-1, 1]), (N, 8, 16, 1, 1)) * rng.integers(120, 128, (N, 8, 16, J, S + far)); a = rng.integers(0, 256, (N, 8, 16, J, 1))
    xb = a - np.add.accumulate(step[..., :S], axis=4); xp = a + np.add.accumulate(step[..., S:], axis=4)
    x = np.concatenate([a.reshape(N, 8, 16, J), xb.reshape(N, 8, 16, J * S), xp.reshape(N, 8, 16, J * far)], axis=3) & 255
    for q in range(N):
        for g in (0, 1, 3, 4, 6, 7):
            w = ids[q, g]; phi[q, g][:, w] = x[q, g]
            nb[q, g][:, w] = np.stack([w[lo], w[hi], w[lo], w[hi]][:D])
    deep(rng, phi, nb, snd, 2); late(rng, nb, 5)
    return pack(phi, mix(rng, nb, 0.0, 0.0), snd)
def setup_inputs_ties(rng):
    phi, nb, snd = parts(rng); v = np.arange(V)
    t = rng.choice(np.array([0, 1, 127, 128, 129, 255]), (N, 8, 16, 6)); phi = np.take_along_axis(t, rng.integers(0, 6, (N, 8, 1, V)), 3)
    nb = mix(rng, nb, 0.2, rng.choice(np.array([0.0, 0.05, 0.15]), (N, 8, 1, 1)))
    nb[:, 1::2, 1] = nb[:, 1::2, 0]; nb[:, 2, 0] = v
    nb[:, 4] = np.minimum(v + rng.integers(0, 5, (N, D, V)), V - 1)
    return pack(phi, nb, snd)
def setup_inputs_ring(rng):
    phi, nb, snd = parts(rng)
    share = np.stack([rng.permutation(np.array([0.0, 0.0, 0.3, 0.3, 0.7, 0.7, 1.0, 1.0])) for q in range(N)]).reshape(N, 8, 1, 1)
    nb = mix(rng, nb, 0.1 * (share < 0.9), share)
    snd[:, ::2] = rng.choice(np.array([0, V - 1, V // 2, 3]), (N, 4, G)); snd[:, 1, 0] = 0; snd[:, 1, G - 1] = V - 1
    nb[:, 3] = rng.choice(np.array([0, V - 1, V, V + G - 1]), (N, D, V))
    top = V - V // 16; snd[:, 5] = rng.integers(top, V, (N, G))
    high = np.where(rng.random((N, D, V)) < 0.5, rng.integers(V, V + G, (N, D, V)), rng.integers(top, V, (N, D, V)))
    nb[:, 5] = np.where(np.arange(V) < top, high, rng.integers(0, 16, (N, D, V)))
    return pack(phi, nb, snd)
def setup_inputs_spread(rng):
    phi, nb, snd = parts(rng)
    phi = np.minimum((np.exp2(8 * rng.random((N, 8, 1, V))) * rng.random((N, 8, 16, V))).astype(np.int64), 255)
    hub = np.minimum(((V + G) * rng.random(nb.shape) ** 3).astype(np.int64), V + G - 1)
    nb = mix(rng, np.where(rng.random(nb.shape) < rng.choice(np.array([0.1, 0.3, 0.6]), (N, 8, 1, 1)), hub, nb), 0.0, 0.05)
    snd = np.minimum((V * rng.random((N, 8, G)) ** 2).astype(np.int64), V - 1)
    return pack(phi, nb, snd)
def check_inputs(d):
    bad = []
    for k, lo, hi in (("phi", 0, 255), ("nb", 0, V + G - 1), ("snd", 0, V - 1)):
        a = np.asarray(d[k]).astype(np.float64)
        if not (np.min(a) >= lo and np.max(a) <= hi): bad.append("range of " + k)
    a = np.asarray(d["phi"]).astype(np.float64)
    if not np.all(a == np.floor(a)): bad.append("whole numbers in phi")
    return bad
def narrow(t, ix):
    return np.take_along_axis(t, ix, 2)
def broad(t, ix):
    return np.take_along_axis(t, ix[:, :, None, :], 3)
def absolute(r, k, gk, gb):
    gh = r >= V; c = np.where(gh, r - V, 0)
    return k + np.where(gh[:, :, None, :], broad(gk, c), 0), np.where(gh, narrow(gb, c), N * r + np.arange(N).reshape(N, 1, 1))
def reference(phi, nb, snd):
    p = phi.astype(np.float32).astype(np.int64).reshape(N, 8, 16, V); nbl = nb.astype(np.int64).reshape(N, 8, D, V)
    sl = np.stack([gentries(a) for a in snd]).astype(np.int64); before = (np.arange(N) - 1) % N
    own = np.zeros((N, 8, V), np.int64) + np.arange(V); slot = np.zeros((N, 8, G), np.int64) + np.arange(V, V + G)
    num = N * own + np.arange(N).reshape(N, 1, 1); none = np.zeros((N, 8, 16, G), np.int64); BIG = 2 ** 40
    r, k, s = own.copy(), np.zeros((N, 8, 16, V), np.int64), own.copy(); ks, b = k.copy(), num.copy()
    gp = broad(p, sl)[before]
    for rnd in range(RO):
        gk, gb = broad(ks, sl)[before], narrow(b, sl)[before]
        ks, b = absolute(r, k, gk, gb)
        uw = np.concatenate([p + 256 * ks, gp + 256 * gk], axis=3); bw = np.concatenate([b, gb], axis=2)
        rw = np.concatenate([r, slot], axis=2); kw = np.concatenate([k, none], axis=3); sw = np.concatenate([ks, gk], axis=3)
        us = broad(uw, s); cj = np.full((N, 8, V), BIG); cw = cj.copy(); uj = np.zeros((N, 8, V), np.int64); ww = uj.copy()
        for i in range(D):
            u = narrow(nbl[:, :, i], s); c = np.add.reduce(np.abs(broad(uw, u) - us), axis=2)
            t = (narrow(bw, u) < num) & (c < cj); cj = np.where(t, c, cj); uj = np.where(t, u, uj)
            t = (narrow(rw, u) == own) & (c < cw); cw = np.where(t, c, cw); ww = np.where(t, u, ww)
        root = r == own; join = root & (cj < BIG)
        o = ((broad(uw, uj) - us + 128) >> 8) + broad(kw, uj) - broad(sw, uj)
        pw = np.concatenate([np.where(join, narrow(rw, uj), r), slot], axis=2)
        ow = np.concatenate([np.where(join[:, :, None, :], o, k), none], axis=3)
        s = np.where(root & ~join & (cw < BIG), ww, s)
        r, k = own.copy(), np.zeros((N, 8, 16, V), np.int64)
        for step in range(S):
            k = k + broad(ow, r); r = narrow(pw, r)
        ks, b = absolute(r, k, gk, gb)
    return {"yk": ks.reshape(N, 128, V).astype(np.float32), "yr": b.astype(np.float32)}

@@ -1,0 +1,512 @@
+from concourse.mybir import AluOpType as A, ActivationFunctionType as F
+
+V, G, W = 2048, 256, 2304
+BF, FP, I32, U16 = "bfloat16", "float32", "int32", "uint16"
+SB = {
+    "ph": (V, BF), "pw": (W, BF), "pc2": (V, BF), "pcs": (V, FP), "tab": (2 * V + W, FP), "ab0": (V, FP), "ab1": (V, FP),
+    "d0": (V, BF), "r0": (V, BF), "g1": (V, BF), "ah1": (V, BF), "xb": (V, FP),
+    "o1a": (W, BF), "o1": (W, BF), "o2": (W, BF), "o4": (W, BF), "o4f": (W, FP), "od": (V, BF), "od2": (V, BF),
+    "tb": (V, FP), "us": (V, FP), "gpe": (G, FP),
+    "nt1": (W, BF), "nt2": (W, BF), "nt3": (W, BF), "wa": (W, BF), "wb": (W, BF), "wc": (W, BF), "wd": (W, BF),
+    "nbt": (W, BF), "n0": (V, BF), "n1": (V, BF), "ns": (V, BF), "dl2": (W, BF), "dl3": (W, BF),
+    "sk1": (G, BF), "sk2": (G, BF), "sk3": (G, BF), "sb2": (G, BF), "sb3": (G, BF), "sbt": (G, BF), "sq": (G, BF),
+    "pre": (G, BF), "idc": (G, BF), "id1": (G, BF),
+    "jj": (272, FP), "j9": (16, FP), "pi": (8, I32), "col": (32, FP), "oh": (16, FP), "bt": (16, FP),
+    "nx": (256, FP), "x4": (128, FP), "nr": (256, FP), "eq": (128, FP),
+    "fr": (144, BF), "fb": (144, BF), "fn": (144, BF), "rb": (16, BF),
+    "wp": (8, FP), "wm": (8, FP), "wph": (8, BF), "wmh": (8, BF),
+    "idf": (128, FP), "inf": (128, FP), "idh": (128, BF), "idn": (128, BF), "zh": (256, BF),
+    "p1": (128, BF), "m1": (128, BF), "p2": (128, BF), "m2": (128, BF), "m4": (128, BF), "ph2": (128, BF),
+    "sni": (16, I32), "snp": (16, I32), "ls": (16, U16), "lp": (16, U16), "lq": (16, U16),
+    "trn": (256, FP), "lnb": (256, U16), "lu": (256, U16),
+    "l1": (144, U16), "l2": (128, U16), "l4": (128, U16), "lr": (144, U16), "sel": (128, U16), "lsc": (128, U16),
+    "e": (256, BF), "jn": (128, BF), "a1": (256, FP), "m": (256, FP), "dm": (128, FP), "t2": (128, BF), "ms": (128, FP),
+    "t": (128, BF), "mt": (128, FP), "w": (256, BF), "md": (256, FP), "mdd": (128, FP), "yrs": (128, FP),
+}
+SCRATCH = {n: ("sbuf", [128, c], d) for n, (c, d) in SB.items()}
+SCRATCH["nba"] = ("sbuf", [128, 2, 8, 16], I32)
+SCRATCH["nbi"] = ("sbuf", [128, 8, 32], FP)
+PS = {"pa": 512, "pb": 512, "pc": 512, "pd": 512, "pt": 2048}
+for _n, _c in PS.items():
+    SCRATCH[_n] = ("psum", [128, _c], FP)
+NDMA = 16
+SEMAPHORES = ["pe", "dve", "act", "pool", "sent"] + ["d%d" % i for i in range(NDMA)] + \
+    ["ak1", "ak2", "ak3", "ab1", "ab2", "ab3"]
+M = 4096.0
+EPS = 1.0 / 512
+OFF = 192.0
+MAGIC = 1.5 * 2 ** 23
+D1 = 1024
+YK = (0, 256, 768, 1280, 1792, V)
+ORDER = """
+0 3 4 1 2 5 10 12 11 64 6 21 56 9 13 49 19 115 8 51 20 17 48 15 47 14 45 32 16 107 7 33 50 59 52 18 113 35 28 60 22 23
+128 30v 24 26v 25 34 31 41 40 27 69 42 36 29 38 37 39 54 43 53 58 67 55 44 84 74 76 82 75 101 102 86 81 87 78 57 79 46
+93 71 83 80 77 106 155p 94 111 103v 185 104 110v 88 121 96 116 105 122 95 112 108 92 118 89 90 124 123 117 109 100 119
+194 114 144 126 125 97 129 120 127 132 98 130 135 131 138 133 145 134 136 99 139 68 137 140 191 141 230 65 142 70 85 91
+154v 143 146 149 188 147 148 150v 151v 156 153v 159 160 157 152v 165p 158 163 164 161 168 162 167p 166v 171 172 169 175
+186 189 176 187 177 180v 190 173 178 170 181 179 192 61 195 182 197 183 216 174 184 200 193 198 196 327 66 199 63 201
+204 330 205 209 202 291p 206 213 217 207 212 203 210 215 211 214 231 218 224 220v 221 239 227 225 208 233 222 226 228
+232 229 219v 234 241 223 240 235 236 62 73 242 237 250 251 238 252 247 243 253 290v 248 244 249 245 257 246 254 258 259
+72 255 256 260 261 262 266 263 264 265 321 267 284 324 283 268 285 269 289p 282 288 296v 287p 272 286p 271 299 297 292
+298 302p 295 303 293 308 300v 301p 294 311 304 309 307 331 273 305 328 312 275v 270 313 322 310 332 316 325 278 314 323
+306 315v 326 317 352 319 337 318 336 320 274 338 329v 277 279 340 280 276 333 339 347 406p 346 350 334 341 351 335 345
+348 281 349 369 366 342 355 353 343 354 367 357 344 356 375 364 368 358 359 370 377 376 371 361v 372 378 373 362v 374
+363 379 360v 380 407 383 365 384 381 385 387 382 386 388 391 389 390 392 393 394 396 395 397 398 400 399 401 403p 402v
+405p 411 404 408 415 416p 412 409 417v 419p 410 423 418 413 420 414 431p 427 428 421 424 422 434p 440 442 441 437 425
+429 443 426 446 432 430 444 447 435 433 438v 436 445 448 439 450v 451 449
+"""
+
+
+def choose(steps):
+    plan = []
+    for x in ORDER.split():
+        i = int(x.rstrip("vp"))
+        alts = steps[i]["alts"]
+        plan.append((i, {"v": "dve", "p": "pool"}.get(x[-1], "act" if "act" in alts else list(alts)[0])))
+    return 0, plan
+
+
+def rank_program(g, core, T, topo):
+    rank = T.rank_of(core)
+    if rank is None:
+        return
+    n = len(T.cores)
+    nxt, prv = T.cores[(rank + 1) % n], T.cores[(rank - 1) % n]
+    Q = {"pe": g.tensor, "dve": g.vector, "act": g.scalar, "pool": g, "sp": g.sync}
+    steps, log = [], {}
+
+    def ap(d):
+        return T[d[0]][:, d[1]:d[2]:d[3]] if len(d) > 3 else T[d[0]][:, d[1]:d[2]]
+
+    def size(d):
+        return len(range(d[1], d[2], d[3])) if len(d) > 3 else d[2] - d[1]
+
+    def two(*ds):
+        return all(d[0] in SB and SB[d[0]][1] in (BF, U16) for d in ds)
+
+    def step(alts, reads, writes, sem=None):
+        me, deps = len(steps), set()
+        for ds, wr in ((reads, False), (writes, True)):
+            for d in ds:
+                lo, hi, w = d[1], d[2], wr
+                if d[0] in PS:
+                    lo, hi, w = (lo // 512) * 512, ((hi + 511) // 512) * 512, True
+                old = log.get(d[0], [])
+                deps.update(x[3] for x in old if x[0] < hi and lo < x[1] and (w or x[2]) and x[3] != me)
+                if w:
+                    old = [x for x in old if not (lo <= x[0] and x[1] <= hi)]
+                log[d[0]] = old + [(lo, hi, w, me)]
+        steps.append({"alts": alts, "deps": sorted(deps), "sem": sem})
+
+    def src(d):
+        if len(d) == 2:
+            return ap(d[0]).indirect(ap(d[1])), [d[0], d[1]], True
+        return ap(d), [d], False
+
+    def sc(x):
+        return (ap(x), [x]) if isinstance(x, tuple) else (x, [])
+
+    def v_cp(out, in_):
+        a, r, ga = src(in_)
+        k = ("g", size(out)) if ga else ("v", size(out) * (0.5 if two(out, in_) else 1))
+        return (lambda: [g.vector.tensor_copy(ap(out), a)], k), r
+
+    def v_ts(out, in0, s1, o0, s2=None, o1=None):
+        a, r, ga = src(in0)
+        x, rx = sc(s1)
+        y, ry = sc(s2)
+        k = ("g", size(out)) if ga else ("v", size(out) * (0.5 if two(out, in0) else 1))
+        if o1 is None:
+            return (lambda: [g.vector.tensor_scalar(ap(out), a, x, None, o0)], k), r + rx
+        return (lambda: [g.vector.tensor_scalar(ap(out), a, x, y, o0, o1)], k), r + rx + ry
+
+    def s_ac(out, in_, fn=F.Identity, scale=1.0, bias=0.0):
+        a, r, ga = src(in_)
+        x, rx = sc(scale)
+        y, ry = sc(bias)
+        return (lambda: [g.scalar.activation(ap(out), a, fn, bias=y, scale=x)], ("g" if ga else "v", size(out))), r + rx + ry
+
+    def cp(out, in_):
+        a, r = v_cp(out, in_)
+        step({"dve": a}, r, [out])
+
+    def ts(out, *x):
+        a, r = v_ts(out, *x)
+        step({"dve": a}, r, [out])
+
+    def ac(out, *x, **kw):
+        a, r = s_ac(out, *x, **kw)
+        step({"act": a}, r, [out])
+
+    def tt(out, in0, in1, o):
+        a, r, ga = src(in0)
+        k = ("g", size(out)) if ga else ("v", size(out) * (1 if in0[0] in PS else 2))
+        step({"dve": (lambda: [g.vector.tensor_tensor(ap(out), a, ap(in1), o)], k)}, r + [in1], [out])
+
+    def either(out, in_, add=None, mul=None):
+        if add is not None:
+            a, r = v_ts(out, in_, add[0], A.add)
+            b, s = s_ac(out, in_, bias=add[1])
+        elif mul is not None:
+            a, r = v_ts(out, in_, mul, A.mult)
+            b, s = s_ac(out, in_, scale=mul)
+        else:
+            a, r = v_cp(out, in_)
+            b, s = s_ac(out, in_)
+        alts = {"dve": a, "act": b}
+        if add is None and mul is None and len(in_) == 3 and in_[0] in SB:
+            alts["pool"] = (lambda: [g.affine_select(ap(out), ap(in_), [[0, size(out)]], A.is_ge, 0.0, 0, 0)],
+                            ("iota", size(out) + 20))
+        step(alts, r + s, [out])
+
+    def pe(ms):
+        cyc = sum(max(min(64, size(x[1])), size(x[2])) * (1 if two(x[1]) else 4) + 10 for x in ms)
+        step({"pe": (lambda: [g.tensor.matmul(ap(x[0]), ap(x[1]), ap(x[2]), x[3], x[4]) for x in ms], ("pe", cyc))},
+             [x[1] for x in ms] + [x[2] for x in ms], [x[0] for x in ms])
+
+    def mm(*x):
+        pe([x])
+
+    def iota(out, pattern, base, cm, flt=True, after=()):
+        kw = {"allow_small_or_imprecise_dtypes": True} if flt else {}
+        step({"pool": (lambda: [g.iota(ap(out), pattern, base, cm, **kw)], ("iota", size(out)))}, list(after), [out])
+
+    ndma = [0]
+
+    def dma(q, out, in_, reads, writes, nbytes):
+        step({q: (lambda: [Q[q].dma_start(out, in_)], ("dma", nbytes))}, reads, writes, ("d%d" % ndma[0], 16))
+        ndma[0] += 1
+
+    omask, out_n, in_n = topo.mask(core, nxt), len(topo.engines(core, nxt)), len(topo.engines(prv, core))
+    rid, pid = topo.addr(nxt, core)
+
+    def send(srcd, dstd, sem, extra):
+        step({"pool": (lambda: [g.remote_dma(ap(dstd), ap(srcd), T.sem[sem], T.sem.sent, pid, rid, omask)],
+                       ("rem", extra))}, [srcd], [dstd], (sem, in_n))
+
+    def c(j):
+        return ("col", j, j + 1)
+
+    def o(j):
+        return ("oh", j, j + 1)
+
+    def whole(nm):
+        return (nm, 0, SB[nm][0])
+
+    def half(nm, k):
+        return (nm, 128 * k, 128 * k + 128)
+
+    def lst(nm, lo, hi, off=0):
+        return (nm, off + lo // 16, off + hi // 16)
+
+    def cuts(k, end=V):
+        return [(x, x + k if x + k < V else end) for x in range(0, V, k)]
+
+    H = V // 2
+    HV, QV = cuts(H), cuts(512)
+    Z, IDF, XT = ("zh", 0, 128), whole("idf"), half("nx", 1)
+    PC, PSEL, PP = ("pc", 0, 128), ("pt", 0, 128), ("pt", 512, 640)
+    PAB = ("pa", "pb")
+    pw = (("pa", 0, 64), ("pb", 0, 64))
+    PM, PF, GB, SCL, C1, RC, B2, MR, MB, MN, PG, M23, B1, PE, ME, PS0, M2O = range(17)
+
+    def wrap(ps, tabl, lo, hi, f):
+        pe([(ps, (f, 15 - i, 143 - i), (tabl, lo + i, hi, 16), i == 0, i == 15) for i in range(16)])
+
+    def gather(out, win, ls, off, pieces, **kw):
+        for lo, hi in pieces:
+            either((out, lo, hi), (win, lst(ls, lo, hi, off)), **kw)
+
+    def narrow(k, nr, tabl):
+        mm((PAB[k], 0, 256), whole("inf"), whole(nr), True, False)
+        pe([((PAB[k], i, 256, 16), (tabl, i, V, 16), whole("rb"), False, False) for i in range(16)] +
+           [((PAB[k], 0, 256), Z, whole("zh"), False, True)])
+
+    def cost(tabl, w, i0=0, i1=16):
+        pe([(("pc", i, 128, 16), (tabl, i, V, 16), whole(w), False, False) for i in range(i0, i1)])
+
+    def before(r):
+        for k in range(2):
+            ts(half("e", k), (PAB[k], 0, 128), 0.0, A.is_lt)
+            tt(half("m", k), (PAB[k], 128, 256), half("e", k), A.mult)
+            if r == 1:
+                either(half("a1", k), (PAB[k], 128, 256))
+            if r == 2:
+                ts(half("w", k), (PAB[k], 128, 256), 0.0, A.is_equal)
+        tt(whole("jn"), half("e", 0), half("e", 1), A.max)
+        tt(whole("dm"), half("m", 1), half("m", 0), A.subtract)
+        if r > 1:
+            mm(PSEL, whole("jn"), whole("m1"), False, False)
+        mm(PP, half("m", 0), IDF, False, False)
+        if r == 2:
+            tt(whole("md"), whole("w"), whole("a1"), A.mult)
+            tt(whole("mdd"), half("md", 1), half("md", 0), A.subtract)
+
+    def decide(r):
+        ms = [(PC, whole("p2"), half("e", 0), False, False), (PC, whole("m2"), half("e", 1), False, False)]
+        if r == 2:
+            ms += [(PC, whole("p1"), half("w", 0), False, False), (PC, whole("m1"), half("w", 1), False, False)]
+        pe(ms + [(PC, whole("m4"), whole("jn"), False, True)])
+        ts(whole("t"), PC, -4 * M - EPS, A.is_lt)
+        if r > 1:
+            mm(PSEL, whole("t"), whole("ph2"), False, True)
+        tt(whole("mt"), whole("t"), whole("dm"), A.mult)
+        mm(PP, whole("mt"), IDF, False, True)
+        if r > 1:
+            cp(whole("sel"), PSEL)
+        cp(("l1", 0, 128), PP)
+        if r == 2:
+            ts(whole("t2"), PC, -EPS, A.is_lt)
+            tt(whole("ms"), whole("t2"), whole("mdd"), A.mult)
+            pe([(PC, XT, IDF, True, False), (PC, half("md", 0), IDF, False, False), (PC, whole("ms"), IDF, False, True)])
+            cp(whole("lsc"), PC)
+            gather("ns", whole("nbt"), "lsc", 0, QV)
+            gather("us", ("tab", 2 * V, 2 * V + W), "lsc", 0, QV, add=(-EPS, c(ME)))
+            for k, f in enumerate(("fr", "fn")):
+                wrap(PC, "ns", 0, V, f)
+                cp(half("lu", k), PC)
+
+    def walk(r):
+        last = r == 3
+        nt, o1, o4 = "nt%d" % r, "o1a" if r == 1 else "o1", "o4f" if last else "o4"
+        for lo, hi in HV:
+            if r == 1:
+                tt((o1, lo, hi), (whole("pw"), lst("l1", lo, hi)), ("pcs", lo, hi), A.subtract)
+            else:
+                ts((o1, lo, hi), (whole("tab"), lst("sel", lo, hi)), MAGIC, A.add, -MAGIC, A.add)
+        gather("wb", whole(nt), "l1", 0, cuts(H, W))
+        for lo, hi in QV:
+            either(("od", lo, hi), (o1, lo, hi), add=(-2 * OFF, c(M2O)) if r == 1 else None)
+        either(("wc", V, W), (nt, V, W))
+        either(("wd", V, W), (nt, V, W))
+        for j, (lo, hi) in enumerate(HV):
+            gather("wc", whole("wb"), "l1", 0, [(lo, hi)])
+            wrap(pw[j], "wc", lo, hi, "fr")
+            cp(lst("l2", lo, hi), pw[j])
+            tt(("o2", lo, hi), (whole(o1), lst("l1", lo, hi)), ("od", lo, hi), A.add)
+        for lo, hi in QV:
+            either(("od2", lo, hi), ("o2", lo, hi))
+        for j, (lo, hi) in enumerate(HV):
+            gather("wd", whole("wc"), "l2", 0, [(lo, hi)])
+            wrap(pw[j], "wd", lo, hi, "fr")
+            cp(lst("l4", lo, hi), pw[j])
+            tt((o4, lo, hi), (whole("o2"), lst("l2", lo, hi)), ("od2", lo, hi), A.add)
+        if last:
+            for lo, hi in QV:
+                either(("xb", lo, hi), (o4, lo, hi))
+                gather("wa", whole("wd"), "l4", 0, [(lo, hi)])
+                pe([(("pd", 0, 128), ("fb", 15 - b, 143 - b), ("wa", 128 * b, 128 * b + 128), b == 0, b == 15)
+                    for b in range(lo // 128, hi // 128)])
+            for x, y in zip(YK[:-1], YK[1:]):
+                tt(("ab1", x, y), (whole(o4), lst("l4", x, y)), ("xb", x, y), A.add)
+                dma("sp", T.yk[:, x:y], T.ab1[:, x:y], [("ab1", x, y)], [], -512 * (y - x))
+            either(whole("yrs"), ("pd", 0, 128))
+            dma("act", T.yr[:], T.yrs[:], [whole("yrs")], [], 65536)
+            return
+        sk, sb = "sk%d" % (r + 1), "sb%d" % (r + 1)
+        either(whole("sq"), (("wd", 0, V), whole("ls")))
+        wrap(("pd", 0, 16), "sq", 0, G, "fr")
+        cp(whole("lq"), ("pd", 0, 16))
+        either(whole("sbt"), (whole("wd"), whole("lq")), mul=c(MB))
+        if r == 1:
+            either(whole("pre"), ((o4, 0, V), whole("ls")))
+        else:
+            tt(whole("pre"), ((o4, 0, V), whole("ls")), whole("sk2"), A.subtract)
+        tt(whole(sk), (whole(o4), whole("lq")), whole("pre"), A.add)
+        send(whole(sk), ("dl%d" % (r + 1), V, W), "ak%d" % (r + 1), 0.0)
+        tt(whole(sb), whole("sbt"), whole("idc"), A.add)
+        send(whole(sb), ("nt%d" % (r + 1), V, W), "ab%d" % (r + 1), 0.0)
+        for lo, hi in QV:
+            mm(("pt", lo, hi), whole("idh"), ("pc2", lo, hi), True, False)
+            mm(("pt", lo, hi), whole("idh"), (o4, lo, hi), False, True)
+            either(("xb", lo, hi), ("pt", lo, hi), add=(EPS, c(PE)))
+        for j, (lo, hi) in enumerate(HV):
+            gather("wa", whole("wd"), "l4", 0, [(lo, hi)])
+            wrap(pw[j], "wa", lo, hi, "fr")
+            cp(lst("lr", lo, hi), pw[j])
+            tt(("tb", lo, hi), (whole(o4), lst("l4", lo, hi)), ("xb", lo, hi), A.add)
+        pe([(("pd", i, 128, 16), ("wa", i, V, 16), ("rb", 8, 16), True, True) for i in range(16)])
+        either(half("nr", 1), ("pd", 0, 128))
+        tt(whole("eq"), ("pd", 0, 128), XT, A.is_equal)
+        tt(half("nr", 0), whole("eq"), half("nx", 0), A.mult)
+
+    dma("act", T.sni[:], T.snd[:], [], [whole("sni")], 30000)
+    dma("sp", T.ph[:], T.phi[:], [], [whole("ph")], 524288)
+    for h in range(2):
+        dma("sp", T.nba[:, h], T.nb[h::2, :], [], [("nba", h, h + 1)], 100000)
+    iota(("pi", 0, 1), [[0, 1]], 0, 1, False)
+    iota(("jj", 0, 272), [[1, 272]], -15, 0)
+    iota(("j9", 0, 8), [[256, 8]], 0, 0)
+    send(whole("sni"), whole("snp"), "ab1", 500.0)
+    iota(XT, [[0, 8], [1, 16]], 0, 16)
+    iota(half("nx", 0), [[0, 8], [4, 16]], rank, 64)
+    J = ("jj", 15, 143)
+    j8 = ("jj", 15, 143, 16)
+    ts(("pi", 4, 5), ("pi", 0, 1), 15, A.bitwise_and)
+    cp(c(PF), ("pi", 0, 1))
+    cp(c(PM), ("pi", 4, 5))
+    ts(whole("oh"), ("jj", 15, 31), c(PM), A.is_equal)
+    tt(c(GB), c(PF), c(PM), A.subtract)
+    ts(c(C1), o(2), 4.0, A.mult, o(0), A.add)
+    ts(c(RC), o(4), float(rank), A.mult)
+    ts(c(SCL), o(3), 4.0, A.mult, o(1), A.add)
+    ts(("bt", 0, 8), ("j9", 0, 8), c(C1), A.mult, c(RC), A.add)
+    ts(c(B2), o(0), 2048.0, A.mult)
+    ts(c(M23), o(2), o(3), A.add)
+    ts(IDF, J, c(PF), A.is_equal)
+    ts(c(B1), o(4), float((rank - 1) % n), A.mult, c(B2), A.add)
+
+    def rows(out, scale, bias):
+        a, r = v_ts(out, ("jj", 15, 271), scale, A.mult, bias, A.add)
+        b, s = s_ac(out, ("jj", 15, 271), scale=scale, bias=bias)
+        step({"dve": a, "act": b}, r, [out])
+
+    for a in range(8):
+        rows(("nt1", 256 * a, 256 * a + 256), c(SCL), ("bt", a, a + 1))
+    rows(whole("id1"), o(1), c(B1))
+    rows(whole("idc"), o(1), c(B2))
+    cp(whole("ls"), whole("sni"))
+    for h in range(2):
+        step({"dve": (lambda h=h: [g.vector.tensor_copy(T.nbi[:, :, 16 * h:16 * h + 16], T.nba[:, h])], ("v", 128))},
+             [("nba", h, h + 1)], [("nbi", h, h + 1)])
+    for b in range(8):
+        step({"dve": (lambda b=b: [g.vector.transpose(T.trn[:, b::8], T.nbi[:, b, :])], ("v", 32))},
+             [("nbi", 0, 2)], [("trn", b, b + 1)])
+    ts(c(MB), c(M23), o(4), A.add)
+    ts(c(MR), o(0), o(1), A.add)
+    cp(whole("lnb"), whole("trn"))
+    for nm, s in (("inf", -1.0), ("idn", -1.0), ("idh", 1.0), ("p2", 2 * M), ("m2", -2 * M), ("m4", -4 * M),
+                  ("p1", M), ("m1", -M), ("ph2", M / 2)):
+        either(whole(nm), IDF, mul=s)
+    either(whole("zh"), ("jj", 0, 256), mul=0.0)
+    ts(("rb", 0, 8), j8, c(GB), A.is_equal, c(MB), A.mult)
+    ts(("rb", 8, 16), j8, c(GB), A.is_equal, c(MR), A.mult)
+    for nm, s in (("wph", 1.0), ("wmh", -1.0), ("wm", -1.0), ("wp", 1.0)):
+        ts(whole(nm), j8, c(GB), A.is_equal, s, A.mult)
+    ts(c(MN), o(5), o(6), A.add)
+    ts(c(PG), c(PM), 2048.0, A.add)
+    for j, x in ((PE, EPS), (ME, -EPS), (PS0, -0.5 - OFF - EPS), (M2O, -2 * OFF)):
+        ts(c(j), o(0), 0.0, A.mult, x, A.add)
+    ts(("l1", 128, 144), ("jj", 15, 31), 16.0, A.mult, c(PG), A.add)
+    ts(("lr", 128, 144), ("jj", 15, 31), 16.0, A.mult, c(PG), A.add)
+    for f, mk in (("fr", MR), ("fb", MB), ("fn", MN)):
+        ts((f, 0, 143), ("jj", 0, 143), c(GB), A.is_equal, c(mk), A.mult)
+    ts(whole("sk1"), (whole("ph"), whole("ls")), -128.0, A.add, 1.0 / 256, A.mult)
+    send(whole("sk1"), ("pw", V, W), "ak1", 0.0)
+    ts(("pw", 0, V), whole("ph"), -128.0, A.add, 1.0 / 256, A.mult)
+    ts(whole("pc2"), whole("ph"), -128.0, A.add, 1.0 / 256, A.mult)
+    cp(whole("lp"), whole("snp"))
+    either(whole("sbt"), (("nt1", 0, V), whole("lp")), mul=c(M23))
+    tt(("nt1", V, W), whole("sbt"), whole("id1"), A.add)
+    for lo, hi in QV:
+        a, r1 = v_ts(("pcs", lo, hi), ("ph", lo, hi), 1.0 / 256, A.mult, -0.5 - OFF - EPS, A.add)
+        b, r2 = s_ac(("pcs", lo, hi), ("ph", lo, hi), scale=1.0 / 256, bias=c(PS0))
+        step({"dve": a, "act": b}, r2, [("pcs", lo, hi)])
+    either(whole("gpe"), ("pw", V, W), add=(EPS, c(PE)))
+    iota(("o1a", V, W), [[0, G]], int(OFF), 0, after=[whole("sk1")])
+    for nm in ("o2", "o4", "o1", "nbt", "o4f"):
+        iota((nm, V, W), [[0, G]], 0, 0, after=[whole("sk1")])
+    iota(whole("x4"), [[0, 8], [1, 16]], 4096, 16, after=[whole("sk1")])
+    for nm in ("dl2", "dl3"):
+        for lo, hi in QV:
+            iota((nm, lo, hi), [[0, hi - lo]], 0, 0, after=[whole("sk1")])
+    for nm in ("nt2", "nt3"):
+        dma("sp", T[nm][:, 0:V], T.nt1[:, 0:V], [("nt1", 0, V), whole("sk1")], [(nm, 0, V)], 524288)
+
+    gather("nbt", whole("nt1"), "lnb", 0, QV)
+    narrow(0, "nx", "nbt")
+    gather("n1", whole("nt1"), "lnb", 128, QV)
+    narrow(1, "nx", "n1")
+    mm(PC, Z, Z, True, False)
+    tt(whole("d0"), (whole("pw"), ("lnb", 0, 128)), whole("pc2"), A.subtract)
+    cost("d0", "wph")
+    for lo in range(D1, V, 512):
+        hi = lo + 512
+        ac(("g1", lo, hi), (whole("pw"), lst("lnb", lo, hi, 128)))
+        pe([(("pt", lo, hi), whole("idn"), ("pc2", lo, hi), True, False),
+            (("pt", lo, hi), whole("idh"), ("g1", lo, hi), False, True)])
+        ac(("ah1", lo, hi), ("pt", lo, hi), F.Abs)
+    tt(("g1", 0, D1), (whole("pw"), lst("lnb", 0, D1, 128)), ("pc2", 0, D1), A.subtract)
+    ac(("ah1", 0, D1), ("g1", 0, D1), F.Abs)
+    ts(whole("r0"), whole("d0"), 0.0, A.max, 2.0, A.mult)
+    cost("r0", "wmh")
+    mm(PP, XT, IDF, True, False)
+    before(1)
+    cost("ah1", "wph")
+    decide(1)
+    for x, y in ((5, 0), (6, 1)):
+        dma("sp", T.nbt[x::16, 0:V], T.n1[y::16, :], [whole("n1")], [("nbt", 0, V)], 32768)
+    walk(1)
+
+    for r in (2, 3):
+        uw = ("tab", 2 * V, 2 * V + W)
+        ug = ("tab", 3 * V, 2 * V + W)
+        lu, own, dl = ("lnb", "pc2", "dl2") if r == 2 else ("lu", "us", "dl3")
+        for lo, hi in HV:
+            tt(("tab", 2 * V + lo, 2 * V + hi), (whole(dl), lst("lr", lo, hi)), ("tb", lo, hi), A.add)
+        tt(ug, (dl, V, W), whole("gpe") if r == 2 else ug, A.add)
+        gather("wb", whole("nt%d" % r), "lr", 0, cuts(512, W))
+        mm(PSEL, whole("x4"), IDF, True, False)
+        mm(PP, half("nr", 1), IDF, True, False)
+        gather("n0", whole("wb"), lu, 0, QV)
+        narrow(0, "nr", "n0")
+        gather("n1", whole("wb"), lu, 128, QV)
+        narrow(1, "nr", "n1")
+        mm(PC, Z, Z, True, False)
+        for k, w in enumerate(("wm", "wp")):
+            ab = "ab%d" % k
+            for lo, hi in HV:
+                tt(("tab", k * V + lo, k * V + hi), (uw, lst(lu, lo, hi, 128 * k)), (own, lo, hi), A.subtract)
+                ac((ab, lo, hi), ("tab", k * V + lo, k * V + hi), F.Abs, bias=c(ME))
+            for i0 in range(0, 16, 4):
+                cost(ab, w, i0, i0 + 4)
+        before(r)
+        decide(r)
+        walk(r)
+
+    plan = choose(steps)[1]
+    assert sorted(i for i, q in plan) == list(range(len(steps)))
+    count = {"pe": 0, "dve": 0, "act": 0, "pool": 0}
+    known = {k: {} for k in Q}
+    mark, clock = {}, {}
+
+    def wait(q, sem, val):
+        if known[q].get(sem, 0) >= val:
+            return
+        Q[q].wait_ge(T.sem[sem], val)
+        known[q][sem] = val
+        for s, v in clock.get((sem, val), {}).items():
+            known[q][s] = max(known[q].get(s, 0), v)
+
+    sends = 0
+    for i, q in plan:
+        need = {}
+        for d in steps[i]["deps"]:
+            s, v = mark[d]
+            if not (s == q == "pe"):
+                need[s] = max(need.get(s, 0), v)
+        for s, v in need.items():
+            wait(q, s, v)
+        fn, kind = steps[i]["alts"][q]
+        calls = fn()
+        if kind[0] == "rem":
+            sends += 1
+            mark[i] = steps[i]["sem"]
+            continue
+        if kind[0] == "dma":
+            mark[i] = steps[i]["sem"]
+            calls[0].then_inc(T.sem[mark[i][0]], 16)
+        else:
+            for x in calls:
+                count[q] += 1
+                x.then_inc(T.sem[q], 1)
+            mark[i] = (q, count[q])
+        clock[mark[i]] = dict(known[q])
+    g.wait_ge(T.sem.sent, sends * out_n)
+    for q in ("pe", "dve", "act", "pool"):
+        wait("pool", q, count[q])
+    for i in range(ndma[0]):
+        wait("pool", "d%d" % i, 16)
+    for r in (1, 2, 3):
+        wait("pool", "ak%d" % r, in_n)
+        wait("pool", "ab%d" % r, in_n)

@@ -1,69 +1,60 @@
 from concourse.mybir import AluOpType as A, ActivationFunctionType as F
 
-V, G, W = 2048, 256, 2304
+V, G, W, H = 2048, 256, 2304, 1024
 BF, FP, I32, U16 = "bfloat16", "float32", "int32", "uint16"
+X0 = 2 * H
+XE = X0 + W + G
+ZW = 640
 SB = {
-    "ph": (V, BF), "pw": (W, BF), "pc2": (V, BF), "pcs": (V, FP), "tab": (2 * V + W, FP), "ab0": (V, FP), "ab1": (V, FP),
-    "d0": (V, BF), "r0": (V, BF), "g1": (V, BF), "ah1": (V, BF), "xb": (V, FP),
-    "o1a": (W, BF), "o1": (W, BF), "o2": (W, BF), "o4": (W, BF), "o4f": (W, FP), "od": (V, BF), "od2": (V, BF),
-    "tb": (V, FP), "us": (V, FP), "gpe": (G, FP),
-    "nt1": (W, BF), "nt2": (W, BF), "nt3": (W, BF), "wa": (W, BF), "wb": (W, BF), "wc": (W, BF), "wd": (W, BF),
-    "nbt": (W, BF), "n0": (V, BF), "n1": (V, BF), "ns": (V, BF), "dl2": (W, BF), "dl3": (W, BF),
-    "sk1": (G, BF), "sk2": (G, BF), "sk3": (G, BF), "sb2": (G, BF), "sb3": (G, BF), "sbt": (G, BF), "sq": (G, BF),
-    "pre": (G, BF), "idc": (G, BF), "id1": (G, BF),
-    "jj": (272, FP), "j9": (16, FP), "pi": (8, I32), "col": (32, FP), "oh": (16, FP), "bt": (16, FP),
-    "nx": (256, FP), "x4": (128, FP), "nr": (256, FP), "eq": (128, FP),
-    "fr": (144, BF), "fb": (144, BF), "fn": (144, BF), "rb": (16, BF),
-    "wp": (8, FP), "wm": (8, FP), "wph": (8, BF), "wmh": (8, BF),
-    "idf": (128, FP), "inf": (128, FP), "idh": (128, BF), "idn": (128, BF), "zh": (256, BF),
-    "p1": (128, BF), "m1": (128, BF), "p2": (128, BF), "m2": (128, BF), "m4": (128, BF), "ph2": (128, BF),
-    "sni": (16, I32), "snp": (16, I32), "ls": (16, U16), "lp": (16, U16), "lq": (16, U16),
+    "ph": (W, BF), "ph2": (V, BF), "pc2": (V, BF), "tab": (XE + 2 * H, FP), "tah": (XE + 2 * H, BF),
+    "ab": (4 * H, FP), "abh": (4 * H, BF), "o1i": (W, I32), "odi": (V, I32), "i8": (128, BF), "w2": (16, BF),
+    "tb1": (V, FP), "tb2": (V, FP), "us": (V, FP), "xb": (V, FP), "dl2": (W, BF), "dl3": (W, BF),
+    "o1": (W, BF), "o2": (W, BF), "o4": (W, BF), "o4f": (W, FP), "od": (V, BF), "od2": (V, BF),
+    "nt": (W + G, BF), "nw": (W + G, BF), "wb": (W, BF), "wc": (W, BF), "wd": (W, BF), "wa": (V, BF),
+    "nbt": (V, BF), "n0": (V, BF), "n1": (V, BF), "ns": (V, BF),
+    "sk1": (G, BF), "sk2": (G, BF), "sk3": (G, BF), "sb2": (G, BF), "sb3": (G, BF),
+    "gb1": (G, BF), "gb2": (G, BF), "gb3": (G, BF),
+    "sq": (G, BF), "pre": (G, BF), "idc": (G, BF), "id1": (G, BF), "base": (G, BF),
+    "jj": (272, FP), "pi": (8, I32), "col": (24, FP), "oh": (16, FP), "bt": (8, FP), "eq8": (8, FP), "eqf": (144, FP),
+    "thr": (256, FP), "c16": (320, BF), "pm": (64, BF), "cd": (384, BF), "lrf": (128, FP),
+    "fr": (144, BF), "fb": (144, BF), "fn": (144, BF), "rx": (24, BF), "r0": (32, BF), "r1": (16, BF),
+    "wf": (16, FP), "wh": (16, BF),
+    "idf": (128, FP), "idh": (128, BF), "pe0": (128, BF), "pe1": (128, BF), "pw0": (128, BF), "pw1": (128, BF),
+    "sa": (128, BF), "sb": (128, BF), "st": (128, BF),
+    "sni": (16, I32), "snp": (16, I32), "ls0": (16, U16), "ls": (16, U16), "lp": (16, U16), "lq": (16, U16),
     "trn": (256, FP), "lnb": (256, U16), "lu": (256, U16),
-    "l1": (144, U16), "l2": (128, U16), "l4": (128, U16), "lr": (144, U16), "sel": (128, U16), "lsc": (128, U16),
-    "e": (256, BF), "jn": (128, BF), "a1": (256, FP), "m": (256, FP), "dm": (128, FP), "t2": (128, BF), "ms": (128, FP),
-    "t": (128, BF), "mt": (128, FP), "w": (256, BF), "md": (256, FP), "mdd": (128, FP), "yrs": (128, FP),
+    "sl": (256, U16), "l2": (128, U16), "l4": (128, U16), "lr": (128, U16), "lsc": (128, U16),
+    "e": (256, BF), "w": (256, BF), "ts": (256, BF), "keep": (256, FP), "yrs": (128, FP),
 }
+PADS = {"jtA": BF, "jrA": FP, "jtB": BF, "jrB": FP, "mv": FP}
 SCRATCH = {n: ("sbuf", [128, c], d) for n, (c, d) in SB.items()}
+for _n, _d in PADS.items():
+    SCRATCH[_n] = ("sbuf", [128, 33, 8], _d)
 SCRATCH["nba"] = ("sbuf", [128, 2, 8, 16], I32)
 SCRATCH["nbi"] = ("sbuf", [128, 8, 32], FP)
-PS = {"pa": 512, "pb": 512, "pc": 512, "pd": 512, "pt": 2048}
-for _n, _c in PS.items():
-    SCRATCH[_n] = ("psum", [128, _c], FP)
-NDMA = 16
-SEMAPHORES = ["pe", "dve", "act", "pool", "sent"] + ["d%d" % i for i in range(NDMA)] + \
-    ["ak1", "ak2", "ak3", "ab1", "ab2", "ab3"]
+PS = ("k0", "k1", "pdA", "pdB", "pcA", "pcB", "plA", "plB")
+for _n in PS:
+    SCRATCH[_n] = ("psum", [128, 8, 64] if _n[1] == "d" else [128, 512], FP)
+NDMA = 40
+ARRIVE = ["a0", "ak1", "ak2", "ak3", "ab2", "ab3"]
+SEMAPHORES = ["pe", "dve", "act", "pool", "sent"] + ARRIVE + ["d%d" % i for i in range(NDMA)]
 M = 4096.0
 EPS = 1.0 / 512
-OFF = 192.0
 MAGIC = 1.5 * 2 ** 23
-D1 = 1024
-YK = (0, 256, 768, 1280, 1792, V)
-ORDER = """
-0 3 4 1 2 5 10 12 11 64 6 21 56 9 13 49 19 115 8 51 20 17 48 15 47 14 45 32 16 107 7 33 50 59 52 18 113 35 28 60 22 23
-128 30v 24 26v 25 34 31 41 40 27 69 42 36 29 38 37 39 54 43 53 58 67 55 44 84 74 76 82 75 101 102 86 81 87 78 57 79 46
-93 71 83 80 77 106 155p 94 111 103v 185 104 110v 88 121 96 116 105 122 95 112 108 92 118 89 90 124 123 117 109 100 119
-194 114 144 126 125 97 129 120 127 132 98 130 135 131 138 133 145 134 136 99 139 68 137 140 191 141 230 65 142 70 85 91
-154v 143 146 149 188 147 148 150v 151v 156 153v 159 160 157 152v 165p 158 163 164 161 168 162 167p 166v 171 172 169 175
-186 189 176 187 177 180v 190 173 178 170 181 179 192 61 195 182 197 183 216 174 184 200 193 198 196 327 66 199 63 201
-204 330 205 209 202 291p 206 213 217 207 212 203 210 215 211 214 231 218 224 220v 221 239 227 225 208 233 222 226 228
-232 229 219v 234 241 223 240 235 236 62 73 242 237 250 251 238 252 247 243 253 290v 248 244 249 245 257 246 254 258 259
-72 255 256 260 261 262 266 263 264 265 321 267 284 324 283 268 285 269 289p 282 288 296v 287p 272 286p 271 299 297 292
-298 302p 295 303 293 308 300v 301p 294 311 304 309 307 331 273 305 328 312 275v 270 313 322 310 332 316 325 278 314 323
-306 315v 326 317 352 319 337 318 336 320 274 338 329v 277 279 340 280 276 333 339 347 406p 346 350 334 341 351 335 345
-348 281 349 369 366 342 355 353 343 354 367 357 344 356 375 364 368 358 359 370 377 376 371 361v 372 378 373 362v 374
-363 379 360v 380 407 383 365 384 381 385 387 382 386 388 391 389 390 392 393 394 396 395 397 398 400 399 401 403p 402v
-405p 411 404 408 415 416p 412 409 417v 419p 410 423 418 413 420 414 431p 427 428 421 424 422 434p 440 442 441 437 425
-429 443 426 446 432 430 444 447 435 433 438v 436 445 448 439 450v 451 449
-"""
+BIG, MID = 8192.0, 1152
+YK = (0, 512, 1024, 1536, 1792, V)
 
-
-def choose(steps):
-    plan = []
-    for x in ORDER.split():
-        i = int(x.rstrip("vp"))
-        alts = steps[i]["alts"]
-        plan.append((i, {"v": "dve", "p": "pool"}.get(x[-1], "act" if "act" in alts else list(alts)[0])))
-    return 0, plan
+ORDER = {1: """
+fill const oB oA B0A D0A B1A scaled iB iA D1A a0A x0A eA a1A x1A D0B B0B B1B tA D1B a0B x0B TA eB kA a1B x1B mA bA sA tB
+mB pc cA TB bB cB sB L2A dA 2A L2B MB 2B L4A dB MA kB nbt 4A L4B u U hA hB S 4B wB wA later yB LB LA HA HB FA v yA G nB
+8B nA FB 8A WA lB lA NA WB g f NB
+"""}
+ONLY = {"k": 1, "const": 1, "pc": 1, "scaled": 1, "fill": 1, "later": 1, "nbt": 1, "m": 2, "M": 2, "n": 2, "N": 2, "w": 2, "F": 3, "H": 3}
+ONWARD = "y h LA LB 8 u U S v G g W f l".split()
+PATH = {"2A": "vv", "2B": "vv", "4A": "vv", "4B": "vv", "8A": "vv", "8B": "vv"}
+COPY = {"sA": "dd", "2A": "dp", "4A": "ss", "sB": "pd", "2B": "dd", "4B": "sp", "sA1": "dd", "sB1": "dd",
+        "bB": "sv", "hB": "vs", "nA": "vs", "nB": "vv", "B0B": "vs", "B1A": "sv",
+        "B0A1": "sv", "B1A1": "ss", "B0B1": "ss", "a0A1": "v", "a1A1": "v"}
 
 
 def rank_program(g, core, T, topo):
@@ -73,116 +64,119 @@ def rank_program(g, core, T, topo):
     n = len(T.cores)
     nxt, prv = T.cores[(rank + 1) % n], T.cores[(rank - 1) % n]
     Q = {"pe": g.tensor, "dve": g.vector, "act": g.scalar, "pool": g, "sp": g.sync}
-    steps, log = [], {}
+    log, mark, clock = {}, [], {}
+    count = {"pe": 0, "dve": 0, "act": 0, "pool": 0, "dma": 0, "rem": 0}
+    known = {k: {} for k in Q}
 
     def ap(d):
+        if d[0][:2] == "pd":
+            a, b = d[1] // 64, d[2] // 64
+            if len(d) == 3:
+                return T[d[0]][:, a:b]
+            return T[d[0]][:, a:b, d[1] % 64::8] if d[3] == 8 else T[d[0]][:, a:b:d[3] // 64]
         return T[d[0]][:, d[1]:d[2]:d[3]] if len(d) > 3 else T[d[0]][:, d[1]:d[2]]
 
-    def size(d):
-        return len(range(d[1], d[2], d[3])) if len(d) > 3 else d[2] - d[1]
+    def wait(q, sem, val):
+        if known[q].get(sem, 0) >= val:
+            return
+        Q[q].wait_ge(T.sem[sem], val)
+        known[q][sem] = val
+        for s, v in clock.get((sem, val), {}).items():
+            known[q][s] = max(known[q].get(s, 0), v)
 
-    def two(*ds):
-        return all(d[0] in SB and SB[d[0]][1] in (BF, U16) for d in ds)
-
-    def step(alts, reads, writes, sem=None):
-        me, deps = len(steps), set()
+    def step(q, calls, reads, writes, sem=None):
+        me, need = len(mark), {}
         for ds, wr in ((reads, False), (writes, True)):
             for d in ds:
-                lo, hi, w = d[1], d[2], wr
-                if d[0] in PS:
-                    lo, hi, w = (lo // 512) * 512, ((hi + 511) // 512) * 512, True
+                ps = d[0] in PS
+                lo, hi = (0, 512) if ps or d[0] in PADS else (d[1], d[2])
                 old = log.get(d[0], [])
-                deps.update(x[3] for x in old if x[0] < hi and lo < x[1] and (w or x[2]) and x[3] != me)
-                if w:
+                for x in old:
+                    if x[0] < hi and lo < x[1] and x[3] != me and (wr or x[2] or (ps and x[4] != q)):
+                        s, v = mark[x[3]]
+                        if not s == q == "pe":
+                            need[s] = max(need.get(s, 0), v)
+                if wr:
                     old = [x for x in old if not (lo <= x[0] and x[1] <= hi)]
-                log[d[0]] = old + [(lo, hi, w, me)]
-        steps.append({"alts": alts, "deps": sorted(deps), "sem": sem})
+                log[d[0]] = old + [(lo, hi, wr, me, q)]
+        for s, v in need.items():
+            wait(q, s, v)
+        done = calls()
+        if sem is None:
+            for x in done:
+                count[q] += 1
+                x.then_inc(T.sem[q], 1)
+            sem = (q, count[q])
+        elif done:
+            done[0].then_inc(T.sem[sem[0]], sem[1])
+        mark.append(sem)
+        if done:
+            clock[sem] = dict(known[q])
 
     def src(d):
-        if len(d) == 2:
-            return ap(d[0]).indirect(ap(d[1])), [d[0], d[1]], True
-        return ap(d), [d], False
+        return (ap(d[0]).indirect(ap(d[1])), [d[0], d[1]]) if len(d) == 2 else (ap(d), [d])
 
     def sc(x):
         return (ap(x), [x]) if isinstance(x, tuple) else (x, [])
 
-    def v_cp(out, in_):
-        a, r, ga = src(in_)
-        k = ("g", size(out)) if ga else ("v", size(out) * (0.5 if two(out, in_) else 1))
-        return (lambda: [g.vector.tensor_copy(ap(out), a)], k), r
-
-    def v_ts(out, in0, s1, o0, s2=None, o1=None):
-        a, r, ga = src(in0)
-        x, rx = sc(s1)
-        y, ry = sc(s2)
-        k = ("g", size(out)) if ga else ("v", size(out) * (0.5 if two(out, in0) else 1))
-        if o1 is None:
-            return (lambda: [g.vector.tensor_scalar(ap(out), a, x, None, o0)], k), r + rx
-        return (lambda: [g.vector.tensor_scalar(ap(out), a, x, y, o0, o1)], k), r + rx + ry
-
-    def s_ac(out, in_, fn=F.Identity, scale=1.0, bias=0.0):
-        a, r, ga = src(in_)
-        x, rx = sc(scale)
-        y, ry = sc(bias)
-        return (lambda: [g.scalar.activation(ap(out), a, fn, bias=y, scale=x)], ("g" if ga else "v", size(out))), r + rx + ry
-
     def cp(out, in_):
-        a, r = v_cp(out, in_)
-        step({"dve": a}, r, [out])
+        a, r = src(in_)
+        step("dve", lambda: [g.vector.tensor_copy(ap(out), a)], r, [out])
 
-    def ts(out, *x):
-        a, r = v_ts(out, *x)
-        step({"dve": a}, r, [out])
-
-    def ac(out, *x, **kw):
-        a, r = s_ac(out, *x, **kw)
-        step({"act": a}, r, [out])
+    def ts(out, in0, s1, o0, s2=None, o1=None):
+        (a, r), (x, rx), (y, ry) = src(in0), sc(s1), sc(s2)
+        ops = (o0,) if o1 is None else (o0, o1)
+        step("dve", lambda: [g.vector.tensor_scalar(ap(out), a, x, y, *ops)], r + rx + ry, [out])
 
     def tt(out, in0, in1, o):
-        a, r, ga = src(in0)
-        k = ("g", size(out)) if ga else ("v", size(out) * (1 if in0[0] in PS else 2))
-        step({"dve": (lambda: [g.vector.tensor_tensor(ap(out), a, ap(in1), o)], k)}, r + [in1], [out])
+        a, r = src(in0)
+        step("dve", lambda: [g.vector.tensor_tensor(ap(out), a, ap(in1), o)], r + [in1], [out])
 
-    def either(out, in_, add=None, mul=None):
-        if add is not None:
-            a, r = v_ts(out, in_, add[0], A.add)
-            b, s = s_ac(out, in_, bias=add[1])
-        elif mul is not None:
-            a, r = v_ts(out, in_, mul, A.mult)
-            b, s = s_ac(out, in_, scale=mul)
+    def ac(out, in_, fn=F.Identity, scale=1.0, bias=0.0):
+        (a, r), (x, rx), (y, ry) = src(in_), sc(scale), sc(bias)
+        step("act", lambda: [g.scalar.activation(ap(out), a, fn, bias=y, scale=x)], r + rx + ry, [out])
+
+    def lin(q, out, in_, scale, bias=0.0):
+        if q == "v":
+            ts(out, in_, scale, A.mult, bias, A.add)
         else:
-            a, r = v_cp(out, in_)
-            b, s = s_ac(out, in_)
-        alts = {"dve": a, "act": b}
-        if add is None and mul is None and len(in_) == 3 and in_[0] in SB:
-            alts["pool"] = (lambda: [g.affine_select(ap(out), ap(in_), [[0, size(out)]], A.is_ge, 0.0, 0, 0)],
-                            ("iota", size(out) + 20))
-        step(alts, r + s, [out])
+            ac(out, in_, scale=scale, bias=bias)
 
     def pe(ms):
-        cyc = sum(max(min(64, size(x[1])), size(x[2])) * (1 if two(x[1]) else 4) + 10 for x in ms)
-        step({"pe": (lambda: [g.tensor.matmul(ap(x[0]), ap(x[1]), ap(x[2]), x[3], x[4]) for x in ms], ("pe", cyc))},
+        step("pe", lambda: [g.tensor.matmul(ap(x[0]), ap(x[1]), ap(x[2]), x[3], x[4]) for x in ms],
              [x[1] for x in ms] + [x[2] for x in ms], [x[0] for x in ms])
 
-    def mm(*x):
-        pe([x])
+    def add(ps, terms):
+        pe([(ps, whole("idh"), x, i == 0, i == len(terms) - 1) for i, x in enumerate(terms)])
 
-    def iota(out, pattern, base, cm, flt=True, after=()):
+    def iota(out, pattern, base, cm, flt=True):
         kw = {"allow_small_or_imprecise_dtypes": True} if flt else {}
-        step({"pool": (lambda: [g.iota(ap(out), pattern, base, cm, **kw)], ("iota", size(out)))}, list(after), [out])
+        step("pool", lambda: [g.iota(ap(out), pattern, base, cm, **kw)], [], [out])
 
-    ndma = [0]
+    def dma(q, out, in_, reads, writes):
+        step(q, lambda: [Q[q].dma_start(out, in_)], reads, writes, ("d%d" % count["dma"], 16))
+        count["dma"] += 1
 
-    def dma(q, out, in_, reads, writes, nbytes):
-        step({q: (lambda: [Q[q].dma_start(out, in_)], ("dma", nbytes))}, reads, writes, ("d%d" % ndma[0], 16))
-        ndma[0] += 1
+    def copy(q, out, in_):
+        if q == "v":
+            cp(out, in_)
+        elif q == "s":
+            ac(out, in_)
+        elif q == "d":
+            dma("sp", ap(out), ap(in_), [in_], [out])
+        else:
+            step("pool", lambda: [g.affine_select(ap(out), ap(in_), [[0, out[2] - out[1]]], A.is_ge, 0.0, 0, 0)],
+                 [in_], [out])
 
     omask, out_n, in_n = topo.mask(core, nxt), len(topo.engines(core, nxt)), len(topo.engines(prv, core))
     rid, pid = topo.addr(nxt, core)
 
-    def send(srcd, dstd, sem, extra):
-        step({"pool": (lambda: [g.remote_dma(ap(dstd), ap(srcd), T.sem[sem], T.sem.sent, pid, rid, omask)],
-                       ("rem", extra))}, [srcd], [dstd], (sem, in_n))
+    def send(srcd, dstd, sem):
+        def call():
+            g.remote_dma(ap(dstd), ap(srcd), T.sem[sem], T.sem.sent, pid, rid, omask)
+            return []
+        step("pool", call, [srcd], [dstd], (sem, in_n))
+        count["rem"] += 1
 
     def c(j):
         return ("col", j, j + 1)
@@ -193,320 +187,332 @@ def rank_program(g, core, T, topo):
     def whole(nm):
         return (nm, 0, SB[nm][0])
 
-    def half(nm, k):
-        return (nm, 128 * k, 128 * k + 128)
+    def part(nm, j, k=64, off=0):
+        return (nm, off + k * j, off + k * j + k)
 
-    def lst(nm, lo, hi, off=0):
-        return (nm, off + lo // 16, off + hi // 16)
+    def pad(nm):
+        return (nm, 1, 33, 2)
 
-    def cuts(k, end=V):
-        return [(x, x + k if x + k < V else end) for x in range(0, V, k)]
+    def upto(nm, h):
+        return (nm, 0, G + H * h + H)
 
-    H = V // 2
-    HV, QV = cuts(H), cuts(512)
-    Z, IDF, XT = ("zh", 0, 128), whole("idf"), half("nx", 1)
-    PC, PSEL, PP = ("pc", 0, 128), ("pt", 0, 128), ("pt", 512, 640)
-    PAB = ("pa", "pb")
-    pw = (("pa", 0, 64), ("pb", 0, 64))
-    PM, PF, GB, SCL, C1, RC, B2, MR, MB, MN, PG, M23, B1, PE, ME, PS0, M2O = range(17)
+    IDF = whole("idf")
+    PM, PF, GB, SCL, C0, C1, C2, MR, MB, M23, MN, WN, WX, PE, ME, XB, FIX, PG, ZERO = range(19)
 
-    def wrap(ps, tabl, lo, hi, f):
-        pe([(ps, (f, 15 - i, 143 - i), (tabl, lo + i, hi, 16), i == 0, i == 15) for i in range(16)])
+    def wrap(ps, tabl, f, first=True, last=True):
+        return [(ps, (f, 15 - i, 143 - i), (tabl[0], tabl[1] + i, tabl[2], 16), first and i == 0, last and i == 15)
+                for i in range(16)]
 
-    def gather(out, win, ls, off, pieces, **kw):
-        for lo, hi in pieces:
-            either((out, lo, hi), (win, lst(ls, lo, hi, off)), **kw)
+    def turn(ps, tabl, w, last=False):
+        return [((ps[0], ps[1] + i, ps[2], 8), (tabl[0], tabl[1] + i, tabl[2], 8), w, False, last and i == 7)
+                for i in range(8)]
 
-    def narrow(k, nr, tabl):
-        mm((PAB[k], 0, 256), whole("inf"), whole(nr), True, False)
-        pe([((PAB[k], i, 256, 16), (tabl, i, V, 16), whole("rb"), False, False) for i in range(16)] +
-           [((PAB[k], 0, 256), Z, whole("zh"), False, True)])
+    def unturn(ps, tile, j, ident, last=False):
+        return [(ps, (tile, 16 * j + 1 - x, 16 * j + 17 - x), (ident, x, 128, 2), False, last and x == 1)
+                for x in range(2)]
 
-    def cost(tabl, w, i0=0, i1=16):
-        pe([(("pc", i, 128, 16), (tabl, i, V, 16), whole(w), False, False) for i in range(i0, i1)])
-
-    def before(r):
-        for k in range(2):
-            ts(half("e", k), (PAB[k], 0, 128), 0.0, A.is_lt)
-            tt(half("m", k), (PAB[k], 128, 256), half("e", k), A.mult)
-            if r == 1:
-                either(half("a1", k), (PAB[k], 128, 256))
-            if r == 2:
-                ts(half("w", k), (PAB[k], 128, 256), 0.0, A.is_equal)
-        tt(whole("jn"), half("e", 0), half("e", 1), A.max)
-        tt(whole("dm"), half("m", 1), half("m", 0), A.subtract)
-        if r > 1:
-            mm(PSEL, whole("jn"), whole("m1"), False, False)
-        mm(PP, half("m", 0), IDF, False, False)
-        if r == 2:
-            tt(whole("md"), whole("w"), whole("a1"), A.mult)
-            tt(whole("mdd"), half("md", 1), half("md", 0), A.subtract)
-
-    def decide(r):
-        ms = [(PC, whole("p2"), half("e", 0), False, False), (PC, whole("m2"), half("e", 1), False, False)]
-        if r == 2:
-            ms += [(PC, whole("p1"), half("w", 0), False, False), (PC, whole("m1"), half("w", 1), False, False)]
-        pe(ms + [(PC, whole("m4"), whole("jn"), False, True)])
-        ts(whole("t"), PC, -4 * M - EPS, A.is_lt)
-        if r > 1:
-            mm(PSEL, whole("t"), whole("ph2"), False, True)
-        tt(whole("mt"), whole("t"), whole("dm"), A.mult)
-        mm(PP, whole("mt"), IDF, False, True)
-        if r > 1:
-            cp(whole("sel"), PSEL)
-        cp(("l1", 0, 128), PP)
-        if r == 2:
-            ts(whole("t2"), PC, -EPS, A.is_lt)
-            tt(whole("ms"), whole("t2"), whole("mdd"), A.mult)
-            pe([(PC, XT, IDF, True, False), (PC, half("md", 0), IDF, False, False), (PC, whole("ms"), IDF, False, True)])
-            cp(whole("lsc"), PC)
-            gather("ns", whole("nbt"), "lsc", 0, QV)
-            gather("us", ("tab", 2 * V, 2 * V + W), "lsc", 0, QV, add=(-EPS, c(ME)))
-            for k, f in enumerate(("fr", "fn")):
-                wrap(PC, "ns", 0, V, f)
-                cp(half("lu", k), PC)
-
-    def walk(r):
-        last = r == 3
-        nt, o1, o4 = "nt%d" % r, "o1a" if r == 1 else "o1", "o4f" if last else "o4"
-        for lo, hi in HV:
-            if r == 1:
-                tt((o1, lo, hi), (whole("pw"), lst("l1", lo, hi)), ("pcs", lo, hi), A.subtract)
-            else:
-                ts((o1, lo, hi), (whole("tab"), lst("sel", lo, hi)), MAGIC, A.add, -MAGIC, A.add)
-        gather("wb", whole(nt), "l1", 0, cuts(H, W))
-        for lo, hi in QV:
-            either(("od", lo, hi), (o1, lo, hi), add=(-2 * OFF, c(M2O)) if r == 1 else None)
-        either(("wc", V, W), (nt, V, W))
-        either(("wd", V, W), (nt, V, W))
-        for j, (lo, hi) in enumerate(HV):
-            gather("wc", whole("wb"), "l1", 0, [(lo, hi)])
-            wrap(pw[j], "wc", lo, hi, "fr")
-            cp(lst("l2", lo, hi), pw[j])
-            tt(("o2", lo, hi), (whole(o1), lst("l1", lo, hi)), ("od", lo, hi), A.add)
-        for lo, hi in QV:
-            either(("od2", lo, hi), ("o2", lo, hi))
-        for j, (lo, hi) in enumerate(HV):
-            gather("wd", whole("wc"), "l2", 0, [(lo, hi)])
-            wrap(pw[j], "wd", lo, hi, "fr")
-            cp(lst("l4", lo, hi), pw[j])
-            tt((o4, lo, hi), (whole("o2"), lst("l2", lo, hi)), ("od2", lo, hi), A.add)
-        if last:
-            for lo, hi in QV:
-                either(("xb", lo, hi), (o4, lo, hi))
-                gather("wa", whole("wd"), "l4", 0, [(lo, hi)])
-                pe([(("pd", 0, 128), ("fb", 15 - b, 143 - b), ("wa", 128 * b, 128 * b + 128), b == 0, b == 15)
-                    for b in range(lo // 128, hi // 128)])
-            for x, y in zip(YK[:-1], YK[1:]):
-                tt(("ab1", x, y), (whole(o4), lst("l4", x, y)), ("xb", x, y), A.add)
-                dma("sp", T.yk[:, x:y], T.ab1[:, x:y], [("ab1", x, y)], [], -512 * (y - x))
-            either(whole("yrs"), ("pd", 0, 128))
-            dma("act", T.yr[:], T.yrs[:], [whole("yrs")], [], 65536)
-            return
-        sk, sb = "sk%d" % (r + 1), "sb%d" % (r + 1)
-        either(whole("sq"), (("wd", 0, V), whole("ls")))
-        wrap(("pd", 0, 16), "sq", 0, G, "fr")
-        cp(whole("lq"), ("pd", 0, 16))
-        either(whole("sbt"), (whole("wd"), whole("lq")), mul=c(MB))
-        if r == 1:
-            either(whole("pre"), ((o4, 0, V), whole("ls")))
-        else:
-            tt(whole("pre"), ((o4, 0, V), whole("ls")), whole("sk2"), A.subtract)
-        tt(whole(sk), (whole(o4), whole("lq")), whole("pre"), A.add)
-        send(whole(sk), ("dl%d" % (r + 1), V, W), "ak%d" % (r + 1), 0.0)
-        tt(whole(sb), whole("sbt"), whole("idc"), A.add)
-        send(whole(sb), ("nt%d" % (r + 1), V, W), "ab%d" % (r + 1), 0.0)
-        for lo, hi in QV:
-            mm(("pt", lo, hi), whole("idh"), ("pc2", lo, hi), True, False)
-            mm(("pt", lo, hi), whole("idh"), (o4, lo, hi), False, True)
-            either(("xb", lo, hi), ("pt", lo, hi), add=(EPS, c(PE)))
-        for j, (lo, hi) in enumerate(HV):
-            gather("wa", whole("wd"), "l4", 0, [(lo, hi)])
-            wrap(pw[j], "wa", lo, hi, "fr")
-            cp(lst("lr", lo, hi), pw[j])
-            tt(("tb", lo, hi), (whole(o4), lst("l4", lo, hi)), ("xb", lo, hi), A.add)
-        pe([(("pd", i, 128, 16), ("wa", i, V, 16), ("rb", 8, 16), True, True) for i in range(16)])
-        either(half("nr", 1), ("pd", 0, 128))
-        tt(whole("eq"), ("pd", 0, 128), XT, A.is_equal)
-        tt(half("nr", 0), whole("eq"), half("nx", 0), A.mult)
-
-    dma("act", T.sni[:], T.snd[:], [], [whole("sni")], 30000)
-    dma("sp", T.ph[:], T.phi[:], [], [whole("ph")], 524288)
+    dma("act", T.sni[:], T.snd[:], [], [whole("sni")])
+    dma("sp", T.ph[:, 0:V], T.phi[:], [], [("ph", 0, V)])
     for h in range(2):
-        dma("sp", T.nba[:, h], T.nb[h::2, :], [], [("nba", h, h + 1)], 100000)
+        dma("sp", T.nba[:, h], T.nb[h::2, :], [], [("nba", h, h + 1)])
+    dma("sp", T.ph2[:], T.phi[:], [], [whole("ph2")])
     iota(("pi", 0, 1), [[0, 1]], 0, 1, False)
     iota(("jj", 0, 272), [[1, 272]], -15, 0)
-    iota(("j9", 0, 8), [[256, 8]], 0, 0)
-    send(whole("sni"), whole("snp"), "ab1", 500.0)
-    iota(XT, [[0, 8], [1, 16]], 0, 16)
-    iota(half("nx", 0), [[0, 8], [4, 16]], rank, 64)
-    J = ("jj", 15, 143)
-    j8 = ("jj", 15, 143, 16)
+    send(whole("sni"), whole("snp"), "a0")
+    iota(("tah", X0, X0 + ZW), [[0, ZW]], 0, 0)
+    J, J256, j8 = ("jj", 15, 143), ("jj", 15, 271), ("jj", 15, 143, 16)
     ts(("pi", 4, 5), ("pi", 0, 1), 15, A.bitwise_and)
     cp(c(PF), ("pi", 0, 1))
     cp(c(PM), ("pi", 4, 5))
-    ts(whole("oh"), ("jj", 15, 31), c(PM), A.is_equal)
     tt(c(GB), c(PF), c(PM), A.subtract)
-    ts(c(C1), o(2), 4.0, A.mult, o(0), A.add)
-    ts(c(RC), o(4), float(rank), A.mult)
+    ts(whole("oh"), ("jj", 15, 31), c(PM), A.is_equal)
     ts(c(SCL), o(3), 4.0, A.mult, o(1), A.add)
-    ts(("bt", 0, 8), ("j9", 0, 8), c(C1), A.mult, c(RC), A.add)
-    ts(c(B2), o(0), 2048.0, A.mult)
-    ts(c(M23), o(2), o(3), A.add)
+    lin("s", c(C2), o(2), 4.0, o(0))
+    lin("s", c(C1), c(C2), 256.0)
+    ts(whole("base"), J256, c(SCL), A.mult)
+    lin("s", c(C2), o(0), 256.0)
+    lin("s", c(C0), o(4), float(rank), c(C2))
+    lin("s", whole("bt"), ("jj", 15, 23), c(C1), c(C0))
+    cp(whole("ls0"), whole("sni"))
     ts(IDF, J, c(PF), A.is_equal)
-    ts(c(B1), o(4), float((rank - 1) % n), A.mult, c(B2), A.add)
-
-    def rows(out, scale, bias):
-        a, r = v_ts(out, ("jj", 15, 271), scale, A.mult, bias, A.add)
-        b, s = s_ac(out, ("jj", 15, 271), scale=scale, bias=bias)
-        step({"dve": a, "act": b}, r, [out])
-
+    for j, x in ((XB, EPS - 0.5), (PE, EPS), (ME, -EPS)):
+        ts(c(j), o(0), 0.0, A.mult, x, A.add)
     for a in range(8):
-        rows(("nt1", 256 * a, 256 * a + 256), c(SCL), ("bt", a, a + 1))
-    rows(whole("id1"), o(1), c(B1))
-    rows(whole("idc"), o(1), c(B2))
-    cp(whole("ls"), whole("sni"))
+        lin("vvvsvvvs"[a], part("nt", a, G, G), whole("base"), 1.0, part("bt", a, 1))
+    for j, x, y, z in ((M23, o(2), 1.0, o(3)), (MR, o(0), 1.0, o(1)), (FIX, o(4), float((rank - 1) % n), 0.0),
+                       (MB, o(4), 1.0, c(M23)), (WN, c(MR), -1.0, 0.0), (WX, c(MR), -BIG, 0.0)):
+        lin("s", c(j), x, y, z)
+    lin("s", whole("idh"), IDF, 1.0)
+    lin("s", whole("id1"), whole("base"), o(1), c(FIX))
+    ts(whole("eq8"), j8, c(GB), A.is_equal)
+    ts(("eqf", 0, 143), ("jj", 0, 143), c(GB), A.is_equal)
+    ts(c(PG), c(PM), float(G), A.add)
+    cp(whole("sk1"), (("ph", 0, V), whole("ls0")))
+    send(whole("sk1"), ("ph", V, W), "ak1")
+    cp(whole("lp"), whole("snp"))
+    ac(whole("gb1"), (("nt", G, W), whole("lp")), scale=c(M23))
     for h in range(2):
-        step({"dve": (lambda h=h: [g.vector.tensor_copy(T.nbi[:, :, 16 * h:16 * h + 16], T.nba[:, h])], ("v", 128))},
+        step("dve", lambda h=h: [g.vector.tensor_copy(T.nbi[:, :, 16 * h:16 * h + 16], T.nba[:, h])],
              [("nba", h, h + 1)], [("nbi", h, h + 1)])
     for b in range(8):
-        step({"dve": (lambda b=b: [g.vector.transpose(T.trn[:, b::8], T.nbi[:, b, :])], ("v", 32))},
-             [("nbi", 0, 2)], [("trn", b, b + 1)])
-    ts(c(MB), c(M23), o(4), A.add)
-    ts(c(MR), o(0), o(1), A.add)
-    cp(whole("lnb"), whole("trn"))
-    for nm, s in (("inf", -1.0), ("idn", -1.0), ("idh", 1.0), ("p2", 2 * M), ("m2", -2 * M), ("m4", -4 * M),
-                  ("p1", M), ("m1", -M), ("ph2", M / 2)):
-        either(whole(nm), IDF, mul=s)
-    either(whole("zh"), ("jj", 0, 256), mul=0.0)
-    ts(("rb", 0, 8), j8, c(GB), A.is_equal, c(MB), A.mult)
-    ts(("rb", 8, 16), j8, c(GB), A.is_equal, c(MR), A.mult)
-    for nm, s in (("wph", 1.0), ("wmh", -1.0), ("wm", -1.0), ("wp", 1.0)):
-        ts(whole(nm), j8, c(GB), A.is_equal, s, A.mult)
-    ts(c(MN), o(5), o(6), A.add)
-    ts(c(PG), c(PM), 2048.0, A.add)
-    for j, x in ((PE, EPS), (ME, -EPS), (PS0, -0.5 - OFF - EPS), (M2O, -2 * OFF)):
-        ts(c(j), o(0), 0.0, A.mult, x, A.add)
-    ts(("l1", 128, 144), ("jj", 15, 31), 16.0, A.mult, c(PG), A.add)
-    ts(("lr", 128, 144), ("jj", 15, 31), 16.0, A.mult, c(PG), A.add)
-    for f, mk in (("fr", MR), ("fb", MB), ("fn", MN)):
-        ts((f, 0, 143), ("jj", 0, 143), c(GB), A.is_equal, c(mk), A.mult)
-    ts(whole("sk1"), (whole("ph"), whole("ls")), -128.0, A.add, 1.0 / 256, A.mult)
-    send(whole("sk1"), ("pw", V, W), "ak1", 0.0)
-    ts(("pw", 0, V), whole("ph"), -128.0, A.add, 1.0 / 256, A.mult)
-    ts(whole("pc2"), whole("ph"), -128.0, A.add, 1.0 / 256, A.mult)
-    cp(whole("lp"), whole("snp"))
-    either(whole("sbt"), (("nt1", 0, V), whole("lp")), mul=c(M23))
-    tt(("nt1", V, W), whole("sbt"), whole("id1"), A.add)
-    for lo, hi in QV:
-        a, r1 = v_ts(("pcs", lo, hi), ("ph", lo, hi), 1.0 / 256, A.mult, -0.5 - OFF - EPS, A.add)
-        b, r2 = s_ac(("pcs", lo, hi), ("ph", lo, hi), scale=1.0 / 256, bias=c(PS0))
-        step({"dve": a, "act": b}, r2, [("pcs", lo, hi)])
-    either(whole("gpe"), ("pw", V, W), add=(EPS, c(PE)))
-    iota(("o1a", V, W), [[0, G]], int(OFF), 0, after=[whole("sk1")])
-    for nm in ("o2", "o4", "o1", "nbt", "o4f"):
-        iota((nm, V, W), [[0, G]], 0, 0, after=[whole("sk1")])
-    iota(whole("x4"), [[0, 8], [1, 16]], 4096, 16, after=[whole("sk1")])
-    for nm in ("dl2", "dl3"):
-        for lo, hi in QV:
-            iota((nm, lo, hi), [[0, hi - lo]], 0, 0, after=[whole("sk1")])
-    for nm in ("nt2", "nt3"):
-        dma("sp", T[nm][:, 0:V], T.nt1[:, 0:V], [("nt1", 0, V), whole("sk1")], [(nm, 0, V)], 524288)
+        step("dve", lambda b=b: [g.vector.transpose(T.trn[:, b::8], T.nbi[:, b, :])], [("nbi", 0, 2)], [("trn", b, b + 1)])
+    step("dve", lambda: [g.vector.tensor_copy(T.lnb[:], T.trn[:])], [("trn", 0, 8)], [whole("lnb")])
 
-    gather("nbt", whole("nt1"), "lnb", 0, QV)
-    narrow(0, "nx", "nbt")
-    gather("n1", whole("nt1"), "lnb", 128, QV)
-    narrow(1, "nx", "n1")
-    mm(PC, Z, Z, True, False)
-    tt(whole("d0"), (whole("pw"), ("lnb", 0, 128)), whole("pc2"), A.subtract)
-    cost("d0", "wph")
-    for lo in range(D1, V, 512):
-        hi = lo + 512
-        ac(("g1", lo, hi), (whole("pw"), lst("lnb", lo, hi, 128)))
-        pe([(("pt", lo, hi), whole("idn"), ("pc2", lo, hi), True, False),
-            (("pt", lo, hi), whole("idh"), ("g1", lo, hi), False, True)])
-        ac(("ah1", lo, hi), ("pt", lo, hi), F.Abs)
-    tt(("g1", 0, D1), (whole("pw"), lst("lnb", 0, D1, 128)), ("pc2", 0, D1), A.subtract)
-    ac(("ah1", 0, D1), ("g1", 0, D1), F.Abs)
-    ts(whole("r0"), whole("d0"), 0.0, A.max, 2.0, A.mult)
-    cost("r0", "wmh")
-    mm(PP, XT, IDF, True, False)
-    before(1)
-    cost("ah1", "wph")
-    decide(1)
-    for x, y in ((5, 0), (6, 1)):
-        dma("sp", T.nbt[x::16, 0:V], T.n1[y::16, :], [whole("n1")], [("nbt", 0, V)], 32768)
-    walk(1)
+    def constants():
+        for nm, wts in (("rx", (c(WN), c(WX), c(WX))), ("r0", (c(MR), c(MB), 0.0, c(WN))), ("r1", (c(MB), c(MR))),
+                        ("wh", (-1.0, 1.0)), ("w2", (-2.0, 2.0))):
+            for j, wt in enumerate(wts):
+                lin("s" if nm[0] == "r" else "v", part(nm, j, 8), whole("eq8"), wt)
 
-    for r in (2, 3):
-        uw = ("tab", 2 * V, 2 * V + W)
-        ug = ("tab", 3 * V, 2 * V + W)
-        lu, own, dl = ("lnb", "pc2", "dl2") if r == 2 else ("lu", "us", "dl3")
-        for lo, hi in HV:
-            tt(("tab", 2 * V + lo, 2 * V + hi), (whole(dl), lst("lr", lo, hi)), ("tb", lo, hi), A.add)
-        tt(ug, (dl, V, W), whole("gpe") if r == 2 else ug, A.add)
-        gather("wb", whole("nt%d" % r), "lr", 0, cuts(512, W))
-        mm(PSEL, whole("x4"), IDF, True, False)
-        mm(PP, half("nr", 1), IDF, True, False)
-        gather("n0", whole("wb"), lu, 0, QV)
-        narrow(0, "nr", "n0")
-        gather("n1", whole("wb"), lu, 128, QV)
-        narrow(1, "nr", "n1")
-        mm(PC, Z, Z, True, False)
-        for k, w in enumerate(("wm", "wp")):
-            ab = "ab%d" % k
-            for lo, hi in HV:
-                tt(("tab", k * V + lo, k * V + hi), (uw, lst(lu, lo, hi, 128 * k)), (own, lo, hi), A.subtract)
-                ac((ab, lo, hi), ("tab", k * V + lo, k * V + hi), F.Abs, bias=c(ME))
-            for i0 in range(0, 16, 4):
-                cost(ab, w, i0, i0 + 4)
-        before(r)
-        decide(r)
-        walk(r)
+    def scaled():
+        lin("s", part("pm", 0), ("jj", 0, 64), 0.0, c(PM))
+        for h in range(2):
+            lin("s", part("lrf", h), ("jj", 15 + 64 * h, 79 + 64 * h), 16.0, c(PG))
+        for nm, s in (("pe0", 4 * M), ("pe1", -8 * M), ("sa", -float(X0 + G)), ("sb", float(W - H)), ("st", float(H))):
+            lin("s", whole(nm), IDF, s)
+        lin("s", ("fr", 0, 143), ("eqf", 0, 143), c(MR))
 
-    plan = choose(steps)[1]
-    assert sorted(i for i, q in plan) == list(range(len(steps)))
-    count = {"pe": 0, "dve": 0, "act": 0, "pool": 0}
-    known = {k: {} for k in Q}
-    mark, clock = {}, {}
+    def later():
+        for nm, s in (("pw0", M), ("pw1", -2 * M)):
+            lin("s", whole(nm), IDF, s)
+        lin("s", whole("idc"), whole("base"), o(1))
+        lin("s", c(MN), o(5), 1.0, o(6))
+        lin("s", ("fb", 0, 143), ("eqf", 0, 143), c(MB))
+        lin("s", ("fn", 0, 143), ("eqf", 0, 143), c(MN))
+        lin("s", whole("wf"), whole("wh"), 1.0)
+        lin("s", whole("i8"), IDF, 1.0 / 256)
 
-    def wait(q, sem, val):
-        if known[q].get(sem, 0) >= val:
-            return
-        Q[q].wait_ge(T.sem[sem], val)
-        known[q][sem] = val
-        for s, v in clock.get((sem, val), {}).items():
-            known[q][s] = max(known[q].get(s, 0), v)
+    def fills():
+        def zero(names):
+            for nm in names:
+                step("pool", lambda nm=nm: [g.iota(T[nm][:], [[0, 264]], 0, 0, allow_small_or_imprecise_dtypes=True)],
+                     [], [pad(nm)])
+        for lo, hi, x in ((0, 64, 0), (64, 192, int(BIG) * MID), (192, 384, 0)):
+            iota(("cd", lo, hi), [[0, hi - lo]], x, 0)
+        for h in range(2):
+            iota(part("thr", h, 128), [[0, 16], [4 - int(BIG), 8]],
+                 rank + (4 - int(BIG)) * H * h - int(BIG) * (G - MID), 8 * (4 - int(BIG)))
+        for j, x in ((0, X0 + G), (2, H), (4, 0)):
+            iota(part("c16", j), [[16, 64]], x, 0)
+        for z in (part("c16", 1), part("c16", 3)):
+            iota(z, [[0, 64]], 0, 0)
+        for x in range(X0 + ZW, XE, ZW):
+            copy("d", ("tah", x, x + ZW), ("tah", X0, X0 + ZW))
+        zero(("jtA", "jrA", "jtB", "jrB"))
+        iota(("o1i", 0, G), [[0, G]], 0, 0, False)
+        for nm in ("nt", "wb", "wc", "wd"):
+            copy("p", (nm, 0, G), ("nt", W, W + G))
+        for nm in ("o2", "o4", "o1"):
+            copy("d", (nm, 0, G), ("tah", X0, X0 + G))
+        for nm in ("dl2", "dl3"):
+            copy("d", (nm, G, W), ("tah", X0, X0 + V))
+        for z in (("tab", X0, X0 + G), ("o4f", 0, G)):
+            iota(z, [[0, G]], 0, 0)
+        zero(("mv",))
 
-    sends = 0
-    for i, q in plan:
-        need = {}
-        for d in steps[i]["deps"]:
-            s, v = mark[d]
-            if not (s == q == "pe"):
-                need[s] = max(need.get(s, 0), v)
-        for s, v in need.items():
-            wait(q, s, v)
-        fn, kind = steps[i]["alts"][q]
-        calls = fn()
-        if kind[0] == "rem":
-            sends += 1
-            mark[i] = steps[i]["sem"]
-            continue
-        if kind[0] == "dma":
-            mark[i] = steps[i]["sem"]
-            calls[0].then_inc(T.sem[mark[i][0]], 16)
-        else:
-            for x in calls:
-                count[q] += 1
-                x.then_inc(T.sem[q], 1)
-            mark[i] = (q, count[q])
-        clock[mark[i]] = dict(known[q])
-    g.wait_ge(T.sem.sent, sends * out_n)
+    def do(r, name):
+        h = 1 if name[-1] == "B" else 0
+        k = 1 if name[1:2] == "1" else 0
+        last = r == 3
+        x = name[0]
+        dk, ab = XE * h + H * k, ("ab" if r > 1 else "abh", H * (2 * h + k))
+        o4, tb = "o4f" if last else "o4", "tb%d" % r
+        pd, pc, pl, jt, jr = [z + "AB"[h] for z in ("pd", "pc", "pl", "jt", "jr")]
+        PC, PSEL, PP, pw = part(pc, 1), part(pl, 1), part(pl, 2), part(pl, 0)
+        sel, l1 = 128 * h, 128 * h + 64
+        halves = [(j, 2 * h + j) for j in range(2)]
+        nx = r + 1
+        tab, o1, od = ("tah", "o1i", "odi") if r == 1 else ("tab", "o1", "od")
+        relu = r == 1 and COPY.get("a" + name[1:] + "1") == "v"
+        near, gh = (("lu", 128 * h + 64 * k), 0) if last else (("lnb", 128 * k + 64 * h), G)
+
+        def gather(out, win, lst, bias=0.0):
+            qs = COPY.get(name + str(r), COPY.get(name, "ss"))
+            m = 1 if qs[0] == qs[1] else 2
+            for j in range(m):
+                lin(qs[j], part(out[0], m * h + j, H // m, out[1]), (win, part(lst[0], j, 64 // m, lst[1])), 1.0, bias)
+
+        def path(z, j):
+            return "v" if (last and z != "2") or (r == 1 and z == "2") else PATH[z + name[-1]][j]
+
+        def doubled(out, off, win, lst, twin, own, bias=0.0):
+            for j, y in halves:
+                if path(x, j) == "v":
+                    tt(part(out, y, 512, off), (win, part(lst[0], j, 32, lst[1])), part(twin, y, 512), A.add)
+                else:
+                    ps = ("k%d" % j, 0, 512)
+                    ac(part("n0", y, 512), (win, part(lst[0], j, 32, lst[1])))
+                    add(ps, [part(win[0], y, 512, G), part("n0", y, 512)] + [part(z, y, 512) for z in own])
+                    lin(path(x, j).lower(), part(out, y, 512, off), ps, 1.0, bias)
+                yield j, y
+
+        if name == "scaled":
+            scaled()
+        elif name == "const":
+            constants()
+        elif name == "pc":
+            ts(whole("pc2"), whole("ph2"), -128.0, A.add, 1.0 / 256, A.mult)
+            ts(whole("ls"), whole("sni"), float(G), A.add)
+        elif name == "later":
+            later()
+        elif name == "fill":
+            fills()
+        elif name == "nbt":
+            for a, b in ((5, 0), (6, 1)):
+                dma("sp", T.nbt[a::16, :], T.n1[b::16, :], [whole("n1")], [whole("nbt")])
+        elif x == "G":
+            add(("k0", 0, G), [whole("idc" if r else "id1"), whole("gb%d" % nx)])
+            ac(("nt", 0, G) if r else ("nt", W, W + G), ("k0", 0, G))
+            if r:
+                copy("p", ("nw", W, W + G) if r == 1 else ("nw", 0, G), ("nt", 0, G))
+        elif x == "g":
+            xg = ("tab", X0, X0 + G) if r == 2 else ("tab", X0 + W, XE)
+            pe([(("k1", 0, G), whole("i8"), ("ph", V, W), True, False)]
+               + [(("k1", 0, G), whole("idh"), ("dl%d" % j, 0, G), False, j == nx) for j in range(2, nx + 1)])
+            ac(xg, ("k1", 0, G), bias=c(XB))
+        elif x == "f":
+            for nm in ("wb", "wc", "wd"):
+                copy("p", (nm, 0, G), ("nt", 0, G))
+        elif x == "l":
+            tt(part("tab", h, H, X0 + G), (whole("dl%d" % nx), part("lr", h)), part(tb, h, H), A.add)
+        elif x == "W":
+            gather(("nw", G), ("nt", 0, W), ("lr", 64 * h))
+        elif x == "n":
+            gather(("ns", 0), whole("nbt"), ("lsc", 64 * h))
+            pe(wrap(part(pc, 0), part("ns", h, H), "fr") + wrap(part(pc, 1), part("ns", h, H), "fn"))
+        elif x == "N":
+            cp(part("lu", h, 128), part(pc, 0, 128))
+        elif x == "w":
+            gather(("us", 0), whole("tb1"), ("lsc", 64 * h), c(ME))
+        elif x == "D":
+            w = H // (k + 1)
+            win = whole("ph") if r == 1 else ("tab", X0 + gh, X0 + gh + W)
+            for j in range(k + 1):
+                tt(part(tab, j, w, dk), (win, part(near[0], j, w // 16, near[1])),
+                   part(("ph2", "pc2", "us")[r - 1], j, w, H * h), A.subtract)
+        elif x == "a":
+            w = H // (k + 1)
+            if relu:
+                ts(part(ab[0], 0, H, ab[1]), part(tab, 0, H, dk), 0.0, A.max)
+            else:
+                for j in range(k + 1):
+                    ac(part(ab[0], j, w, ab[1]), part(tab, j, w, dk), F.Abs, bias=c(ME) if r > 1 else 0.0)
+        elif x == "x":
+            ms = turn(PC, part(tab, 0, H, dk), part("wh", 1 - k, 8)) if relu else []
+            pe(ms + turn(PC, part(ab[0], 0, H, ab[1]), part("wf" if r > 1 else "w2" if relu else "wh", k, 8), k == 1))
+        elif x == "o":
+            rows = part("nt", h, H, G) if r == 1 else part("wa", h, H)
+            pe([((pc, 0, 192), whole("idh"), ("cd", 192, 384), True, False),
+                ((pd, 0, 256), whole("idh"), ("cd", 0, 256), True, False)] + turn((pd, 0, 192), rows, whole("rx")))
+        elif x == "B":
+            nk = "n1" if k else "nbt" if r == 1 else "n0"
+            gather((nk, 0), ("nt" if r == 1 else "nw", gh, gh + W), near)
+            pe(turn((pd, 128 * k, 256), part(nk, h, H), whole("r%d" % k), k == 1))
+        elif x == "e":
+            tt(part("e", h, 128), (pd, 64, 192), part("thr", h, 128), A.is_lt)
+            ms = [(part(pc, 0), whole("pe1"), part("e", 2 * h + j), False, False) for j in range(2)]
+            ms += [(PC, whole("pe%d" % j), part("e", 2 * h + j), False, False) for j in range(2)]
+            if r == 2:
+                tt(part("w", h, 128), (pd, 64, 192), part("thr", h, 128), A.is_equal)
+                ms += [(part(pc, 2), whole("pw1"), part("w", 2 * h + j), False, False) for j in range(2)]
+                ms += [(PC, whole("pw%d" % j), part("w", 2 * h + j), False, False) for j in range(2)]
+            pe(ms)
+        elif x == "i":
+            pe([((pl, 64, 192), whole("idh"), part("c16", h, 128), True, False),
+                (PSEL, whole("idh"), whole("pm"), False, False), (PP, IDF, part("lrf", h), False, False)])
+        elif x == "t":
+            ts(pad(jt), (pc, 0, 128), -4 * M - EPS, A.is_lt)
+            tt(pad(jr), (pd, 0, 256, 192), pad(jt), A.mult)
+            pe(unturn(PSEL, jt, 0, "sb" if h else "sa") + unturn(PSEL, jt, 1, "st")
+               + unturn(PP, jr, 0, "idf") + unturn(PP, jr, 1, "idf", True))
+            if r == 2:
+                ts(part("ts", h, 128), (pc, 64, 192), -M - EPS, A.is_lt)
+        elif x == "T":
+            cp(part("sl", h, 128), (pl, 64, 192))
+        elif x == "k":
+            for j in range(2):
+                ac(part("keep", 2 * h + j), part(pd, 3 - 3 * j))
+        elif x == "m":
+            tt(pad("mv"), part("ts", h, 128), part("keep", h, 128), A.mult)
+            pe([(part(pc, 0), whole("idh"), part("c16", 2 if h else 4), True, False)]
+               + unturn(part(pc, 0), "mv", 0, "idf") + unturn(part(pc, 0), "mv", 1, "idf", True))
+        elif x == "M":
+            ts(part("lsc", h), part(pc, 0), c(PM), A.add, V - 1.0, A.min)
+        elif x == "s":
+            win = (tab, X0 + G, XE + 2 * H) if h else (tab, 0, X0 + W)
+            ops = (0.5, A.add, 1.0 / 256, A.mult) if r == 1 else (MAGIC, A.add, -MAGIC, A.add)
+            for j, y in halves:
+                ts(part(o1, y, 512, G), (win, part("sl", j, 32, sel)), *ops)
+                if path("2", j) == "v":
+                    copy(COPY[name + "1" * (r == 1)][j], part(od, y, 512), part(o1, y, 512, G))
+        elif x == "b":
+            gather(("wb", G), ("nt", 0, W), ("sl", l1))
+        elif x == "c":
+            gather(("wc", G), upto("wb", h), ("sl", l1))
+            pe(wrap(pw, part("wc", h, H, G), "fr"))
+        elif x == "L":
+            cp(part("l" + (name[1] if len(name) == 3 else "r"), h), pw)
+            if len(name) == 2:
+                ac(part("lrf", h), pw)
+        elif x == "2":
+            for j, y in doubled("o2", G, upto(o1, h), ("sl", l1), od, []):
+                if path("4", j) == "v":
+                    copy(COPY[name][j], part("od2", y, 512), part("o2", y, 512, G))
+        elif x == "d":
+            gather(("wd", G), upto("wc", h), ("l2", 64 * h))
+            pe(wrap(pw, part("wd", h, H, G), "fr"))
+        elif x == "4":
+            for j, y in doubled(o4, G, upto("o2", h), ("l2", 64 * h), "od2", []):
+                if last:
+                    copy(COPY[name][j], part("xb", y, 512), part(o4, y, 512, G))
+        elif x == "y":
+            for j, y in halves:
+                if path("8", j) == "v":
+                    add(("k%d" % j, 0, 512), [part("pc2", y, 512), part(o4, y, 512, G)])
+                    ac(part("xb", y, 512), ("k%d" % j, 0, 512), bias=c(PE))
+        elif x in "hH":
+            gather(("wa", 0), upto("wd", h), ("l4", 64 * h))
+            if last:
+                pe([(("k0", 0, 128), ("fb", 15 - b, 143 - b), part("wa", b, 128), b == 0, b == 15)
+                    for b in range(8 * h, 8 * h + 8)])
+                if h:
+                    ac(whole("yrs"), ("k0", 0, 128))
+                    dma("act", T.yr[:], T.yrs[:], [whole("yrs")], [])
+            else:
+                pe(wrap(pw, part("wa", h, H), "fr"))
+        elif x == "F":
+            for lo, hi in zip(YK[:-1], YK[1:]):
+                if lo // H == h:
+                    tt(("tb1", lo, hi), (upto(o4, h), ("l4", lo // 16, hi // 16)), ("xb", lo, hi), A.add)
+                    dma("sp", T.yk[:, lo:hi], T.tb1[:, lo:hi], [("tb1", lo, hi)], [])
+        elif x == "8":
+            list(doubled(tb, 0, upto(o4, h), ("l4", 64 * h), "xb", ["pc2"], c(PE)))
+        elif x == "u":
+            ac(whole("sq"), (whole("wd"), whole("ls")))
+            pe(wrap(("pcB", 256, 272), whole("sq"), "fr"))
+        elif x == "U":
+            cp(whole("lq"), ("pcB", 256, 272))
+        elif x == "S":
+            ac(whole("sb%d" % nx), (whole("wd"), whole("lq")), scale=c(MB))
+            send(whole("sb%d" % nx), whole("gb%d" % nx), "ab%d" % nx)
+        elif x == "v":
+            if r == 1:
+                cp(whole("pre"), (whole(o4), whole("ls")))
+            else:
+                tt(whole("pre"), (whole(o4), whole("ls")), whole("sk2"), A.subtract)
+            tt(whole("sk%d" % nx), (whole(o4), whole("lq")), whole("pre"), A.add)
+            send(whole("sk%d" % nx), ("dl%d" % nx, 0, G), "ak%d" % nx)
+
+    do(0, "G")
+    for r in (1, 2, 3):
+        for name in ORDER[1].split():
+            if ONLY.get(name, ONLY.get(name[0], r)) == r and not (r == 3 and (name in ONWARD or name[0] in ONWARD)):
+                do(r, name)
+
+    g.wait_ge(T.sem.sent, count["rem"] * out_n)
     for q in ("pe", "dve", "act", "pool"):
         wait("pool", q, count[q])
-    for i in range(ndma[0]):
+    for i in range(count["dma"]):
         wait("pool", "d%d" % i, 16)
-    for r in (1, 2, 3):
-        wait("pool", "ak%d" % r, in_n)
-        wait("pool", "ab%d" % r, in_n)
+    for s in ARRIVE:
+        wait("pool", s, in_n)

from concourse.mybir import AluOpType as A, ActivationFunctionType as F

V, G, W, H = 2048, 256, 2304, 1024
BF, FP, I32, U16 = "bfloat16", "float32", "int32", "uint16"
X0 = 2 * H
XE = X0 + W + G
ZW = 640
SB = {
    "ph": (W, BF), "ph2": (V, BF), "pc2": (V, BF), "tab": (XE + 2 * H, FP), "tah": (XE + 2 * H, BF),
    "ab": (4 * H, FP), "abh": (4 * H, BF), "o1i": (W, I32), "odi": (V, I32), "i8": (128, BF), "w2": (16, BF),
    "tb1": (V, FP), "tb2": (V, FP), "us": (V, FP), "xb": (V, FP), "dl2": (W, BF), "dl3": (W, BF),
    "o1": (W, BF), "o2": (W, BF), "o4": (W, BF), "o4f": (W, FP), "od": (V, BF), "od2": (V, BF),
    "nt": (W + G, BF), "nw": (W + G, BF), "wb": (W, BF), "wc": (W, BF), "wd": (W, BF), "wa": (V, BF),
    "nbt": (V, BF), "n0": (V, BF), "n1": (V, BF), "ns": (V, BF),
    "sk1": (G, BF), "sk2": (G, BF), "sk3": (G, BF), "sb2": (G, BF), "sb3": (G, BF),
    "gb1": (G, BF), "gb2": (G, BF), "gb3": (G, BF),
    "sq": (G, BF), "pre": (G, BF), "idc": (G, BF), "id1": (G, BF), "base": (G, BF),
    "jj": (272, FP), "pi": (8, I32), "col": (24, FP), "oh": (16, FP), "bt": (8, FP), "eq8": (8, FP), "eqf": (144, FP),
    "thr": (256, FP), "c16": (320, BF), "pm": (64, BF), "cd": (384, BF), "lrf": (128, FP),
    "fr": (144, BF), "fb": (144, BF), "fn": (144, BF), "rx": (24, BF), "r0": (32, BF), "r1": (16, BF),
    "wf": (16, FP), "wh": (16, BF),
    "idf": (128, FP), "idh": (128, BF), "pe0": (128, BF), "pe1": (128, BF), "pw0": (128, BF), "pw1": (128, BF),
    "sa": (128, BF), "sb": (128, BF), "st": (128, BF),
    "sni": (16, I32), "snp": (16, I32), "ls0": (16, U16), "ls": (16, U16), "lp": (16, U16), "lq": (16, U16),
    "trn": (256, FP), "lnb": (256, U16), "lu": (256, U16),
    "sl": (256, U16), "l2": (128, U16), "l4": (128, U16), "lr": (128, U16), "lsc": (128, U16),
    "e": (256, BF), "w": (256, BF), "ts": (256, BF), "keep": (256, FP), "yrs": (128, FP),
}
PADS = {"jtA": BF, "jrA": FP, "jtB": BF, "jrB": FP, "mv": FP}
SCRATCH = {n: ("sbuf", [128, c], d) for n, (c, d) in SB.items()}
for _n, _d in PADS.items():
    SCRATCH[_n] = ("sbuf", [128, 33, 8], _d)
SCRATCH["nba"] = ("sbuf", [128, 2, 8, 16], I32)
SCRATCH["nbi"] = ("sbuf", [128, 8, 32], FP)
PS = ("k0", "k1", "pdA", "pdB", "pcA", "pcB", "plA", "plB")
for _n in PS:
    SCRATCH[_n] = ("psum", [128, 8, 64] if _n[1] == "d" else [128, 512], FP)
NDMA = 40
ARRIVE = ["a0", "ak1", "ak2", "ak3", "ab2", "ab3"]
SEMAPHORES = ["pe", "dve", "act", "pool", "sent"] + ARRIVE + ["d%d" % i for i in range(NDMA)]
M = 4096.0
EPS = 1.0 / 512
MAGIC = 1.5 * 2 ** 23
BIG, MID = 8192.0, 1152
YK = (0, 512, 1024, 1536, 1792, V)

ORDER = {1: """
fill const oB oA B0A D0A B1A scaled iB iA D1A a0A x0A eA a1A x1A D0B B0B B1B tA D1B a0B x0B TA eB kA a1B x1B mA bA sA tB
mB pc cA TB bB cB sB L2A dA 2A L2B MB 2B L4A dB MA kB nbt 4A L4B u U hA hB S 4B wB wA later yB LB LA HA HB FA v yA G nB
8B nA FB 8A WA lB lA NA WB g f NB
"""}
ONLY = {"k": 1, "const": 1, "pc": 1, "scaled": 1, "fill": 1, "later": 1, "nbt": 1, "m": 2, "M": 2, "n": 2, "N": 2, "w": 2, "F": 3, "H": 3}
ONWARD = "y h LA LB 8 u U S v G g W f l".split()
PATH = {"2A": "vv", "2B": "vv", "4A": "vv", "4B": "vv", "8A": "vv", "8B": "vv"}
COPY = {"sA": "dd", "2A": "dp", "4A": "ss", "sB": "pd", "2B": "dd", "4B": "sp", "sA1": "dd", "sB1": "dd",
        "bB": "sv", "hB": "vs", "nA": "vs", "nB": "vv", "B0B": "vs", "B1A": "sv",
        "B0A1": "sv", "B1A1": "ss", "B0B1": "ss", "a0A1": "v", "a1A1": "v"}


def rank_program(g, core, T, topo):
    rank = T.rank_of(core)
    if rank is None:
        return
    n = len(T.cores)
    nxt, prv = T.cores[(rank + 1) % n], T.cores[(rank - 1) % n]
    Q = {"pe": g.tensor, "dve": g.vector, "act": g.scalar, "pool": g, "sp": g.sync}
    log, mark, clock = {}, [], {}
    count = {"pe": 0, "dve": 0, "act": 0, "pool": 0, "dma": 0, "rem": 0}
    known = {k: {} for k in Q}

    def ap(d):
        if d[0][:2] == "pd":
            a, b = d[1] // 64, d[2] // 64
            if len(d) == 3:
                return T[d[0]][:, a:b]
            return T[d[0]][:, a:b, d[1] % 64::8] if d[3] == 8 else T[d[0]][:, a:b:d[3] // 64]
        return T[d[0]][:, d[1]:d[2]:d[3]] if len(d) > 3 else T[d[0]][:, d[1]:d[2]]

    def wait(q, sem, val):
        if known[q].get(sem, 0) >= val:
            return
        Q[q].wait_ge(T.sem[sem], val)
        known[q][sem] = val
        for s, v in clock.get((sem, val), {}).items():
            known[q][s] = max(known[q].get(s, 0), v)

    def step(q, calls, reads, writes, sem=None):
        me, need = len(mark), {}
        for ds, wr in ((reads, False), (writes, True)):
            for d in ds:
                ps = d[0] in PS
                lo, hi = (0, 512) if ps or d[0] in PADS else (d[1], d[2])
                old = log.get(d[0], [])
                for x in old:
                    if x[0] < hi and lo < x[1] and x[3] != me and (wr or x[2] or (ps and x[4] != q)):
                        s, v = mark[x[3]]
                        if not s == q == "pe":
                            need[s] = max(need.get(s, 0), v)
                if wr:
                    old = [x for x in old if not (lo <= x[0] and x[1] <= hi)]
                log[d[0]] = old + [(lo, hi, wr, me, q)]
        for s, v in need.items():
            wait(q, s, v)
        done = calls()
        if sem is None:
            for x in done:
                count[q] += 1
                x.then_inc(T.sem[q], 1)
            sem = (q, count[q])
        elif done:
            done[0].then_inc(T.sem[sem[0]], sem[1])
        mark.append(sem)
        if done:
            clock[sem] = dict(known[q])

    def src(d):
        return (ap(d[0]).indirect(ap(d[1])), [d[0], d[1]]) if len(d) == 2 else (ap(d), [d])

    def sc(x):
        return (ap(x), [x]) if isinstance(x, tuple) else (x, [])

    def cp(out, in_):
        a, r = src(in_)
        step("dve", lambda: [g.vector.tensor_copy(ap(out), a)], r, [out])

    def ts(out, in0, s1, o0, s2=None, o1=None):
        (a, r), (x, rx), (y, ry) = src(in0), sc(s1), sc(s2)
        ops = (o0,) if o1 is None else (o0, o1)
        step("dve", lambda: [g.vector.tensor_scalar(ap(out), a, x, y, *ops)], r + rx + ry, [out])

    def tt(out, in0, in1, o):
        a, r = src(in0)
        step("dve", lambda: [g.vector.tensor_tensor(ap(out), a, ap(in1), o)], r + [in1], [out])

    def ac(out, in_, fn=F.Identity, scale=1.0, bias=0.0):
        (a, r), (x, rx), (y, ry) = src(in_), sc(scale), sc(bias)
        step("act", lambda: [g.scalar.activation(ap(out), a, fn, bias=y, scale=x)], r + rx + ry, [out])

    def lin(q, out, in_, scale, bias=0.0):
        if q == "v":
            ts(out, in_, scale, A.mult, bias, A.add)
        else:
            ac(out, in_, scale=scale, bias=bias)

    def pe(ms):
        step("pe", lambda: [g.tensor.matmul(ap(x[0]), ap(x[1]), ap(x[2]), x[3], x[4]) for x in ms],
             [x[1] for x in ms] + [x[2] for x in ms], [x[0] for x in ms])

    def add(ps, terms):
        pe([(ps, whole("idh"), x, i == 0, i == len(terms) - 1) for i, x in enumerate(terms)])

    def iota(out, pattern, base, cm, flt=True):
        kw = {"allow_small_or_imprecise_dtypes": True} if flt else {}
        step("pool", lambda: [g.iota(ap(out), pattern, base, cm, **kw)], [], [out])

    def dma(q, out, in_, reads, writes):
        step(q, lambda: [Q[q].dma_start(out, in_)], reads, writes, ("d%d" % count["dma"], 16))
        count["dma"] += 1

    def copy(q, out, in_):
        if q == "v":
            cp(out, in_)
        elif q == "s":
            ac(out, in_)
        elif q == "d":
            dma("sp", ap(out), ap(in_), [in_], [out])
        else:
            step("pool", lambda: [g.affine_select(ap(out), ap(in_), [[0, out[2] - out[1]]], A.is_ge, 0.0, 0, 0)],
                 [in_], [out])

    omask, out_n, in_n = topo.mask(core, nxt), len(topo.engines(core, nxt)), len(topo.engines(prv, core))
    rid, pid = topo.addr(nxt, core)

    def send(srcd, dstd, sem):
        def call():
            g.remote_dma(ap(dstd), ap(srcd), T.sem[sem], T.sem.sent, pid, rid, omask)
            return []
        step("pool", call, [srcd], [dstd], (sem, in_n))
        count["rem"] += 1

    def c(j):
        return ("col", j, j + 1)

    def o(j):
        return ("oh", j, j + 1)

    def whole(nm):
        return (nm, 0, SB[nm][0])

    def part(nm, j, k=64, off=0):
        return (nm, off + k * j, off + k * j + k)

    def pad(nm):
        return (nm, 1, 33, 2)

    def upto(nm, h):
        return (nm, 0, G + H * h + H)

    IDF = whole("idf")
    PM, PF, GB, SCL, C0, C1, C2, MR, MB, M23, MN, WN, WX, PE, ME, XB, FIX, PG, ZERO = range(19)

    def wrap(ps, tabl, f, first=True, last=True):
        return [(ps, (f, 15 - i, 143 - i), (tabl[0], tabl[1] + i, tabl[2], 16), first and i == 0, last and i == 15)
                for i in range(16)]

    def turn(ps, tabl, w, last=False):
        return [((ps[0], ps[1] + i, ps[2], 8), (tabl[0], tabl[1] + i, tabl[2], 8), w, False, last and i == 7)
                for i in range(8)]

    def unturn(ps, tile, j, ident, last=False):
        return [(ps, (tile, 16 * j + 1 - x, 16 * j + 17 - x), (ident, x, 128, 2), False, last and x == 1)
                for x in range(2)]

    dma("act", T.sni[:], T.snd[:], [], [whole("sni")])
    dma("sp", T.ph[:, 0:V], T.phi[:], [], [("ph", 0, V)])
    for h in range(2):
        dma("sp", T.nba[:, h], T.nb[h::2, :], [], [("nba", h, h + 1)])
    dma("sp", T.ph2[:], T.phi[:], [], [whole("ph2")])
    iota(("pi", 0, 1), [[0, 1]], 0, 1, False)
    iota(("jj", 0, 272), [[1, 272]], -15, 0)
    send(whole("sni"), whole("snp"), "a0")
    iota(("tah", X0, X0 + ZW), [[0, ZW]], 0, 0)
    J, J256, j8 = ("jj", 15, 143), ("jj", 15, 271), ("jj", 15, 143, 16)
    ts(("pi", 4, 5), ("pi", 0, 1), 15, A.bitwise_and)
    cp(c(PF), ("pi", 0, 1))
    cp(c(PM), ("pi", 4, 5))
    tt(c(GB), c(PF), c(PM), A.subtract)
    ts(whole("oh"), ("jj", 15, 31), c(PM), A.is_equal)
    ts(c(SCL), o(3), 4.0, A.mult, o(1), A.add)
    lin("s", c(C2), o(2), 4.0, o(0))
    lin("s", c(C1), c(C2), 256.0)
    ts(whole("base"), J256, c(SCL), A.mult)
    lin("s", c(C2), o(0), 256.0)
    lin("s", c(C0), o(4), float(rank), c(C2))
    lin("s", whole("bt"), ("jj", 15, 23), c(C1), c(C0))
    cp(whole("ls0"), whole("sni"))
    ts(IDF, J, c(PF), A.is_equal)
    for j, x in ((XB, EPS - 0.5), (PE, EPS), (ME, -EPS)):
        ts(c(j), o(0), 0.0, A.mult, x, A.add)
    for a in range(8):
        lin("vvvsvvvs"[a], part("nt", a, G, G), whole("base"), 1.0, part("bt", a, 1))
    for j, x, y, z in ((M23, o(2), 1.0, o(3)), (MR, o(0), 1.0, o(1)), (FIX, o(4), float((rank - 1) % n), 0.0),
                       (MB, o(4), 1.0, c(M23)), (WN, c(MR), -1.0, 0.0), (WX, c(MR), -BIG, 0.0)):
        lin("s", c(j), x, y, z)
    lin("s", whole("idh"), IDF, 1.0)
    lin("s", whole("id1"), whole("base"), o(1), c(FIX))
    ts(whole("eq8"), j8, c(GB), A.is_equal)
    ts(("eqf", 0, 143), ("jj", 0, 143), c(GB), A.is_equal)
    ts(c(PG), c(PM), float(G), A.add)
    cp(whole("sk1"), (("ph", 0, V), whole("ls0")))
    send(whole("sk1"), ("ph", V, W), "ak1")
    cp(whole("lp"), whole("snp"))
    ac(whole("gb1"), (("nt", G, W), whole("lp")), scale=c(M23))
    for h in range(2):
        step("dve", lambda h=h: [g.vector.tensor_copy(T.nbi[:, :, 16 * h:16 * h + 16], T.nba[:, h])],
             [("nba", h, h + 1)], [("nbi", h, h + 1)])
    for b in range(8):
        step("dve", lambda b=b: [g.vector.transpose(T.trn[:, b::8], T.nbi[:, b, :])], [("nbi", 0, 2)], [("trn", b, b + 1)])
    step("dve", lambda: [g.vector.tensor_copy(T.lnb[:], T.trn[:])], [("trn", 0, 8)], [whole("lnb")])

    def constants():
        for nm, wts in (("rx", (c(WN), c(WX), c(WX))), ("r0", (c(MR), c(MB), 0.0, c(WN))), ("r1", (c(MB), c(MR))),
                        ("wh", (-1.0, 1.0)), ("w2", (-2.0, 2.0))):
            for j, wt in enumerate(wts):
                lin("s" if nm[0] == "r" else "v", part(nm, j, 8), whole("eq8"), wt)

    def scaled():
        lin("s", part("pm", 0), ("jj", 0, 64), 0.0, c(PM))
        for h in range(2):
            lin("s", part("lrf", h), ("jj", 15 + 64 * h, 79 + 64 * h), 16.0, c(PG))
        for nm, s in (("pe0", 4 * M), ("pe1", -8 * M), ("sa", -float(X0 + G)), ("sb", float(W - H)), ("st", float(H))):
            lin("s", whole(nm), IDF, s)
        lin("s", ("fr", 0, 143), ("eqf", 0, 143), c(MR))

    def later():
        for nm, s in (("pw0", M), ("pw1", -2 * M)):
            lin("s", whole(nm), IDF, s)
        lin("s", whole("idc"), whole("base"), o(1))
        lin("s", c(MN), o(5), 1.0, o(6))
        lin("s", ("fb", 0, 143), ("eqf", 0, 143), c(MB))
        lin("s", ("fn", 0, 143), ("eqf", 0, 143), c(MN))
        lin("s", whole("wf"), whole("wh"), 1.0)
        lin("s", whole("i8"), IDF, 1.0 / 256)

    def fills():
        def zero(names):
            for nm in names:
                step("pool", lambda nm=nm: [g.iota(T[nm][:], [[0, 264]], 0, 0, allow_small_or_imprecise_dtypes=True)],
                     [], [pad(nm)])
        for lo, hi, x in ((0, 64, 0), (64, 192, int(BIG) * MID), (192, 384, 0)):
            iota(("cd", lo, hi), [[0, hi - lo]], x, 0)
        for h in range(2):
            iota(part("thr", h, 128), [[0, 16], [4 - int(BIG), 8]],
                 rank + (4 - int(BIG)) * H * h - int(BIG) * (G - MID), 8 * (4 - int(BIG)))
        for j, x in ((0, X0 + G), (2, H), (4, 0)):
            iota(part("c16", j), [[16, 64]], x, 0)
        for z in (part("c16", 1), part("c16", 3)):
            iota(z, [[0, 64]], 0, 0)
        for x in range(X0 + ZW, XE, ZW):
            copy("d", ("tah", x, x + ZW), ("tah", X0, X0 + ZW))
        zero(("jtA", "jrA", "jtB", "jrB"))
        iota(("o1i", 0, G), [[0, G]], 0, 0, False)
        for nm in ("nt", "wb", "wc", "wd"):
            copy("p", (nm, 0, G), ("nt", W, W + G))
        for nm in ("o2", "o4", "o1"):
            copy("d", (nm, 0, G), ("tah", X0, X0 + G))
        for nm in ("dl2", "dl3"):
            copy("d", (nm, G, W), ("tah", X0, X0 + V))
        for z in (("tab", X0, X0 + G), ("o4f", 0, G)):
            iota(z, [[0, G]], 0, 0)
        zero(("mv",))

    def do(r, name):
        h = 1 if name[-1] == "B" else 0
        k = 1 if name[1:2] == "1" else 0
        last = r == 3
        x = name[0]
        dk, ab = XE * h + H * k, ("ab" if r > 1 else "abh", H * (2 * h + k))
        o4, tb = "o4f" if last else "o4", "tb%d" % r
        pd, pc, pl, jt, jr = [z + "AB"[h] for z in ("pd", "pc", "pl", "jt", "jr")]
        PC, PSEL, PP, pw = part(pc, 1), part(pl, 1), part(pl, 2), part(pl, 0)
        sel, l1 = 128 * h, 128 * h + 64
        halves = [(j, 2 * h + j) for j in range(2)]
        nx = r + 1
        tab, o1, od = ("tah", "o1i", "odi") if r == 1 else ("tab", "o1", "od")
        relu = r == 1 and COPY.get("a" + name[1:] + "1") == "v"
        near, gh = (("lu", 128 * h + 64 * k), 0) if last else (("lnb", 128 * k + 64 * h), G)

        def gather(out, win, lst, bias=0.0):
            qs = COPY.get(name + str(r), COPY.get(name, "ss"))
            m = 1 if qs[0] == qs[1] else 2
            for j in range(m):
                lin(qs[j], part(out[0], m * h + j, H // m, out[1]), (win, part(lst[0], j, 64 // m, lst[1])), 1.0, bias)

        def path(z, j):
            return "v" if (last and z != "2") or (r == 1 and z == "2") else PATH[z + name[-1]][j]

        def doubled(out, off, win, lst, twin, own, bias=0.0):
            for j, y in halves:
                if path(x, j) == "v":
                    tt(part(out, y, 512, off), (win, part(lst[0], j, 32, lst[1])), part(twin, y, 512), A.add)
                else:
                    ps = ("k%d" % j, 0, 512)
                    ac(part("n0", y, 512), (win, part(lst[0], j, 32, lst[1])))
                    add(ps, [part(win[0], y, 512, G), part("n0", y, 512)] + [part(z, y, 512) for z in own])
                    lin(path(x, j).lower(), part(out, y, 512, off), ps, 1.0, bias)
                yield j, y

        if name == "scaled":
            scaled()
        elif name == "const":
            constants()
        elif name == "pc":
            ts(whole("pc2"), whole("ph2"), -128.0, A.add, 1.0 / 256, A.mult)
            ts(whole("ls"), whole("sni"), float(G), A.add)
        elif name == "later":
            later()
        elif name == "fill":
            fills()
        elif name == "nbt":
            for a, b in ((5, 0), (6, 1)):
                dma("sp", T.nbt[a::16, :], T.n1[b::16, :], [whole("n1")], [whole("nbt")])
        elif x == "G":
            add(("k0", 0, G), [whole("idc" if r else "id1"), whole("gb%d" % nx)])
            ac(("nt", 0, G) if r else ("nt", W, W + G), ("k0", 0, G))
            if r:
                copy("p", ("nw", W, W + G) if r == 1 else ("nw", 0, G), ("nt", 0, G))
        elif x == "g":
            xg = ("tab", X0, X0 + G) if r == 2 else ("tab", X0 + W, XE)
            pe([(("k1", 0, G), whole("i8"), ("ph", V, W), True, False)]
               + [(("k1", 0, G), whole("idh"), ("dl%d" % j, 0, G), False, j == nx) for j in range(2, nx + 1)])
            ac(xg, ("k1", 0, G), bias=c(XB))
        elif x == "f":
            for nm in ("wb", "wc", "wd"):
                copy("p", (nm, 0, G), ("nt", 0, G))
        elif x == "l":
            tt(part("tab", h, H, X0 + G), (whole("dl%d" % nx), part("lr", h)), part(tb, h, H), A.add)
        elif x == "W":
            gather(("nw", G), ("nt", 0, W), ("lr", 64 * h))
        elif x == "n":
            gather(("ns", 0), whole("nbt"), ("lsc", 64 * h))
            pe(wrap(part(pc, 0), part("ns", h, H), "fr") + wrap(part(pc, 1), part("ns", h, H), "fn"))
        elif x == "N":
            cp(part("lu", h, 128), part(pc, 0, 128))
        elif x == "w":
            gather(("us", 0), whole("tb1"), ("lsc", 64 * h), c(ME))
        elif x == "D":
            w = H // (k + 1)
            win = whole("ph") if r == 1 else ("tab", X0 + gh, X0 + gh + W)
            for j in range(k + 1):
                tt(part(tab, j, w, dk), (win, part(near[0], j, w // 16, near[1])),
                   part(("ph2", "pc2", "us")[r - 1], j, w, H * h), A.subtract)
        elif x == "a":
            w = H // (k + 1)
            if relu:
                ts(part(ab[0], 0, H, ab[1]), part(tab, 0, H, dk), 0.0, A.max)
            else:
                for j in range(k + 1):
                    ac(part(ab[0], j, w, ab[1]), part(tab, j, w, dk), F.Abs, bias=c(ME) if r > 1 else 0.0)
        elif x == "x":
            ms = turn(PC, part(tab, 0, H, dk), part("wh", 1 - k, 8)) if relu else []
            pe(ms + turn(PC, part(ab[0], 0, H, ab[1]), part("wf" if r > 1 else "w2" if relu else "wh", k, 8), k == 1))
        elif x == "o":
            rows = part("nt", h, H, G) if r == 1 else part("wa", h, H)
            pe([((pc, 0, 192), whole("idh"), ("cd", 192, 384), True, False),
                ((pd, 0, 256), whole("idh"), ("cd", 0, 256), True, False)] + turn((pd, 0, 192), rows, whole("rx")))
        elif x == "B":
            nk = "n1" if k else "nbt" if r == 1 else "n0"
            gather((nk, 0), ("nt" if r == 1 else "nw", gh, gh + W), near)
            pe(turn((pd, 128 * k, 256), part(nk, h, H), whole("r%d" % k), k == 1))
        elif x == "e":
            tt(part("e", h, 128), (pd, 64, 192), part("thr", h, 128), A.is_lt)
            ms = [(part(pc, 0), whole("pe1"), part("e", 2 * h + j), False, False) for j in range(2)]
            ms += [(PC, whole("pe%d" % j), part("e", 2 * h + j), False, False) for j in range(2)]
            if r == 2:
                tt(part("w", h, 128), (pd, 64, 192), part("thr", h, 128), A.is_equal)
                ms += [(part(pc, 2), whole("pw1"), part("w", 2 * h + j), False, False) for j in range(2)]
                ms += [(PC, whole("pw%d" % j), part("w", 2 * h + j), False, False) for j in range(2)]
            pe(ms)
        elif x == "i":
            pe([((pl, 64, 192), whole("idh"), part("c16", h, 128), True, False),
                (PSEL, whole("idh"), whole("pm"), False, False), (PP, IDF, part("lrf", h), False, False)])
        elif x == "t":
            ts(pad(jt), (pc, 0, 128), -4 * M - EPS, A.is_lt)
            tt(pad(jr), (pd, 0, 256, 192), pad(jt), A.mult)
            pe(unturn(PSEL, jt, 0, "sb" if h else "sa") + unturn(PSEL, jt, 1, "st")
               + unturn(PP, jr, 0, "idf") + unturn(PP, jr, 1, "idf", True))
            if r == 2:
                ts(part("ts", h, 128), (pc, 64, 192), -M - EPS, A.is_lt)
        elif x == "T":
            cp(part("sl", h, 128), (pl, 64, 192))
        elif x == "k":
            for j in range(2):
                ac(part("keep", 2 * h + j), part(pd, 3 - 3 * j))
        elif x == "m":
            tt(pad("mv"), part("ts", h, 128), part("keep", h, 128), A.mult)
            pe([(part(pc, 0), whole("idh"), part("c16", 2 if h else 4), True, False)]
               + unturn(part(pc, 0), "mv", 0, "idf") + unturn(part(pc, 0), "mv", 1, "idf", True))
        elif x == "M":
            ts(part("lsc", h), part(pc, 0), c(PM), A.add, V - 1.0, A.min)
        elif x == "s":
            win = (tab, X0 + G, XE + 2 * H) if h else (tab, 0, X0 + W)
            ops = (0.5, A.add, 1.0 / 256, A.mult) if r == 1 else (MAGIC, A.add, -MAGIC, A.add)
            for j, y in halves:
                ts(part(o1, y, 512, G), (win, part("sl", j, 32, sel)), *ops)
                if path("2", j) == "v":
                    copy(COPY[name + "1" * (r == 1)][j], part(od, y, 512), part(o1, y, 512, G))
        elif x == "b":
            gather(("wb", G), ("nt", 0, W), ("sl", l1))
        elif x == "c":
            gather(("wc", G), upto("wb", h), ("sl", l1))
            pe(wrap(pw, part("wc", h, H, G), "fr"))
        elif x == "L":
            cp(part("l" + (name[1] if len(name) == 3 else "r"), h), pw)
            if len(name) == 2:
                ac(part("lrf", h), pw)
        elif x == "2":
            for j, y in doubled("o2", G, upto(o1, h), ("sl", l1), od, []):
                if path("4", j) == "v":
                    copy(COPY[name][j], part("od2", y, 512), part("o2", y, 512, G))
        elif x == "d":
            gather(("wd", G), upto("wc", h), ("l2", 64 * h))
            pe(wrap(pw, part("wd", h, H, G), "fr"))
        elif x == "4":
            for j, y in doubled(o4, G, upto("o2", h), ("l2", 64 * h), "od2", []):
                if last:
                    copy(COPY[name][j], part("xb", y, 512), part(o4, y, 512, G))
        elif x == "y":
            for j, y in halves:
                if path("8", j) == "v":
                    add(("k%d" % j, 0, 512), [part("pc2", y, 512), part(o4, y, 512, G)])
                    ac(part("xb", y, 512), ("k%d" % j, 0, 512), bias=c(PE))
        elif x in "hH":
            gather(("wa", 0), upto("wd", h), ("l4", 64 * h))
            if last:
                pe([(("k0", 0, 128), ("fb", 15 - b, 143 - b), part("wa", b, 128), b == 0, b == 15)
                    for b in range(8 * h, 8 * h + 8)])
                if h:
                    ac(whole("yrs"), ("k0", 0, 128))
                    dma("act", T.yr[:], T.yrs[:], [whole("yrs")], [])
            else:
                pe(wrap(pw, part("wa", h, H), "fr"))
        elif x == "F":
            for lo, hi in zip(YK[:-1], YK[1:]):
                if lo // H == h:
                    tt(("tb1", lo, hi), (upto(o4, h), ("l4", lo // 16, hi // 16)), ("xb", lo, hi), A.add)
                    dma("sp", T.yk[:, lo:hi], T.tb1[:, lo:hi], [("tb1", lo, hi)], [])
        elif x == "8":
            list(doubled(tb, 0, upto(o4, h), ("l4", 64 * h), "xb", ["pc2"], c(PE)))
        elif x == "u":
            ac(whole("sq"), (whole("wd"), whole("ls")))
            pe(wrap(("pcB", 256, 272), whole("sq"), "fr"))
        elif x == "U":
            cp(whole("lq"), ("pcB", 256, 272))
        elif x == "S":
            ac(whole("sb%d" % nx), (whole("wd"), whole("lq")), scale=c(MB))
            send(whole("sb%d" % nx), whole("gb%d" % nx), "ab%d" % nx)
        elif x == "v":
            if r == 1:
                cp(whole("pre"), (whole(o4), whole("ls")))
            else:
                tt(whole("pre"), (whole(o4), whole("ls")), whole("sk2"), A.subtract)
            tt(whole("sk%d" % nx), (whole(o4), whole("lq")), whole("pre"), A.add)
            send(whole("sk%d" % nx), ("dl%d" % nx, 0, G), "ak%d" % nx)

    do(0, "G")
    for r in (1, 2, 3):
        for name in ORDER[1].split():
            if ONLY.get(name, ONLY.get(name[0], r)) == r and not (r == 3 and (name in ONWARD or name[0] in ONWARD)):
                do(r, name)

    g.wait_ge(T.sem.sent, count["rem"] * out_n)
    for q in ("pe", "dve", "act", "pool"):
        wait("pool", q, count[q])
    for i in range(count["dma"]):
        wait("pool", "d%d" % i, 16)
    for s in ARRIVE:
        wait("pool", s, in_n)
